import numpy as np
import ml_dtypes


def mxq(x, axis, fmt="e4m3"):
    dtype, down = {"e4m3": (ml_dtypes.float8_e4m3fn, 7), "e5m2": (ml_dtypes.float8_e5m2, 14)}[fmt]
    v = np.moveaxis(np.asarray(x, np.float32).astype(ml_dtypes.bfloat16).astype(np.float64), axis, -1)
    blocks = v.reshape(v.shape[:-1] + (-1, 32))
    amax = np.abs(blocks).max(-1, keepdims=True)
    byte = np.maximum(np.where(amax > 0, np.frexp(amax)[1] - 1 + 127, 0) - down, 1)
    scale = np.exp2(byte - 127.0)
    codes = (blocks / scale).astype(np.float32).astype(dtype).astype(np.float64)
    return np.moveaxis((codes * scale).reshape(v.shape), -1, axis)


WIDE = False


def mx_kscale(k):
    if not WIDE:
        return np.ones(k)
    levels = np.array([24, -24, 12, -12, 0])
    if k % 512:
        return np.exp2(np.random.permutation(np.resize(levels, k // 32))).repeat(32)
    a = np.empty((k // 512, 16))
    for p in range(k // 512):
        a[p, :8] = np.random.permutation(np.resize(levels, 8))
        for g in range(8):
            far = levels[np.abs(levels - a[p, g]) >= 10]
            a[p, g + 8] = far[np.random.randint(len(far))]
    return np.exp2(a.ravel()).repeat(32)


def f64(x):
    return np.asarray(x).astype(np.float64)


E2M1 = np.array([0.0, 0.5, 1.0, 1.5, 2.0, 3.0, 4.0, 6.0, -0.0, -0.5, -1.0, -1.5, -2.0, -3.0, -4.0, -6.0])


def pack_weight(w, fmt):
    k, n = w.shape
    w = f64(np.asarray(w, np.float32).astype(ml_dtypes.bfloat16)).reshape(k // 32, 32, n)
    amax = np.abs(w).max(1)
    if fmt == "e4m3":
        byte = np.frexp(amax)[1] - 1 + 127 - 7
    else:
        mant, ex = np.frexp(amax / 6.0)
        byte = np.where(mant > 0.5, ex, ex - 1) + 127
    byte = np.clip(np.where(amax > 0, byte, 1), 1, 254)
    scaled = (w * np.exp2(127.0 - byte)[:, None, :]).reshape(k, n).astype(np.float32)
    by_word = np.ascontiguousarray(scaled.reshape(k // 512, 128, 4, n).transpose(0, 1, 3, 2))
    if fmt == "e4m3":
        words = by_word.astype(ml_dtypes.float8_e4m3fn).view(np.uint8)
    else:
        c = by_word.astype(ml_dtypes.float4_e2m1fn).view(np.uint8) & 0xF
        words = (c[..., 0::2] | (c[..., 1::2] << 4)).reshape(k // 512, 128, 2 * n)
    return np.ascontiguousarray(words), np.ascontiguousarray(byte.astype(np.uint8).reshape(k // 512, 16, n))


def unpack_weight(words, scales, fmt):
    g, _, n = scales.shape
    words = np.ascontiguousarray(words).reshape(g, 128, n, -1)
    if fmt == "e4m3":
        vals = words.view(ml_dtypes.float8_e4m3fn).astype(np.float64)
    else:
        nib = np.empty((g, 128, n, 4), np.uint8)
        nib[..., 0::2] = words & 0xF
        nib[..., 1::2] = words >> 4
        vals = E2M1[nib]
    vals = vals * np.repeat(np.exp2(scales.astype(np.float64) - 127.0), 8, axis=1)[..., None]
    return vals.transpose(0, 1, 3, 2).reshape(g * 512, n)


def planes(y):
    n, m = y.shape
    v = y.astype(np.float32).astype(ml_dtypes.bfloat16).astype(np.float64).reshape(n // 32, 32, m)
    top = np.abs(v).max(1)
    byte = np.clip(np.where(top > 0, np.frexp(top)[1] - 1 + 127 - 7, 1), 1, 254)
    codes = (v * np.exp2(127.0 - byte)[:, None, :]).reshape(n, m).astype(np.float32).astype(ml_dtypes.float8_e4m3fn).view(np.uint8)
    words = codes.reshape(n // 512, 128, 4, m).transpose(0, 1, 3, 2)
    return np.ascontiguousarray(words), np.ascontiguousarray(byte.astype(np.uint8).reshape(n // 512, 16, m))


def sigm(f):
    return 1.0 / (1.0 + np.exp(-np.maximum(f, -700.0)))


K, R, N, T = 512, 512, 512, 1024


def setup_inputs():
    n = np.random.standard_normal
    u = mx_kscale(R)[:, None]
    s = mx_kscale(K)[:, None]
    v = n((R, N)) / np.sqrt(R) / u
    v4 = pack_weight(v, "e2m1")
    vrest = v - unpack_weight(*v4, "e2m1")
    p_wg = pack_weight(n((K, R)) / np.sqrt(K) / s, "e4m3")
    p_v8 = pack_weight(vrest, "e4m3")
    return {
        "x": (n((K, T)) * s).astype(np.float32),
        "wg_words": p_wg[0],
        "wg_scales": p_wg[1],
        "wu": (n((K, R)) / np.sqrt(K) / s * u.T).astype(np.float32),
        "v4_words": v4[0],
        "v4_scales": v4[1],
        "v8_words": p_v8[0],
        "v8_scales": p_v8[1],
        "g": (n((N, T))).astype(np.float32),
    }


def reference(x, wg_words, wg_scales, wu, v4_words, v4_scales, v8_words, v8_scales, g):
    x_ = mxq(f64(x), 0, "e4m3")
    wg_ = unpack_weight(wg_words, wg_scales, "e4m3")
    wu_ = mxq(f64(wu), 0, "e4m3")
    ga = wg_.T @ x_
    ub = wu_.T @ x_
    h = sigm(ga) * ub
    h_ = mxq(h, 0, "e4m3")
    v4_ = unpack_weight(v4_words, v4_scales, "e2m1")
    v8_ = unpack_weight(v8_words, v8_scales, "e4m3")
    y = v4_.T @ h_ + v8_.T @ h_
    return (y * f64(g), h) + planes(h)

@@ -1,0 +1,211 @@
+from contextlib import ExitStack
+
+import concourse.mybir as mybir
+
+K, R, N, T = 512, 512, 512, 1024
+FLOPS = 2 * T * (2 * K * R + 2 * R * N)
+
+F32 = mybir.dt.float32
+BF16 = mybir.dt.bfloat16
+I32 = mybir.dt.int32
+U32 = mybir.dt.uint32
+U8 = mybir.dt.uint8
+FP8X4 = mybir.dt.float8_e4m3fn_x4
+FP4X4 = mybir.dt.float4_e2m1fn_x4
+SIGMOID = mybir.ActivationFunctionType.Sigmoid
+MULT = mybir.AluOpType.mult
+
+P = 128
+PACK = 4
+HALF = T // 2
+QUADS = 4
+
+X0_VECTOR = 320
+WU_VECTOR = 80
+X1_SCALAR = 384
+H0_SCALAR = 256
+
+
+def tile_mix_glusave_sigm_res_mul_kernel(
+    tc, x, wg_words, wg_scales, wu, v4_words, v4_scales, v8_words, v8_scales, g, out_0, out_1, out_2, out_3
+):
+    nc = tc.nc
+    with ExitStack() as ctx:
+        sb = ctx.enter_context(tc.tile_pool(name="sb", bufs=1))
+        ps = ctx.enter_context(tc.psum_pool(name="ps", bufs=1))
+        ctx.enter_context(tc.manual_schedule())
+
+        def tile(name, shape, dtype):
+            return sb.tile(shape, dtype, name=name, align_bytes=64)
+
+        def bank(index, name):
+            return ps.tile([P, HALF], F32, name=name, tag="bank%d" % index)
+
+        x_rows = x.rearrange("(p j) t -> p j t", j=PACK)
+        h_rows = out_1.rearrange("(p j) t -> p j t", j=PACK)
+        g_rows = g.rearrange("(c p) t -> p c t", p=P)
+        y_rows = out_0.rearrange("(c p) t -> p c t", p=P)
+        code_rows = out_2[0].rearrange("p t i -> p (t i)").bitcast(I32)
+
+        wg_raw = tile("wg_raw", [P, R], I32)
+        wg_scale_raw = tile("wg_scale_raw", [P, R], U8)
+        wg_codes = tile("wg_codes", [P, R], I32)
+        wg_scale = tile("wg_scale", [P, R], U8)
+        wu_raw = tile("wu_raw", [P, PACK, R], F32)
+        wu_bf = tile("wu_bf", [P, PACK * R], BF16)
+        wu_codes = tile("wu_codes", [P, R], U32)
+        wu_scale = tile("wu_scale", [P, R], U8)
+        v4_codes = tile("v4_codes", [P, 2 * N], U8)
+        v8_codes = tile("v8_codes", [P, N], U32)
+        v4_scale = tile("v4_scale", [P, N], U8)
+        v8_scale = tile("v8_scale", [P, N], U8)
+        x_raw = [tile("x_raw%d" % s, [P, PACK, HALF], F32) for s in range(2)]
+        x_bf = [tile("x_bf%d" % s, [P, PACK * HALF], BF16) for s in range(2)]
+        x_codes = [tile("x_codes%d" % s, [P, HALF], U32) for s in range(2)]
+        x_scale = [tile("x_scale%d" % s, [P, HALF], U8) for s in range(2)]
+        g_sb = [tile("g_sb%d" % s, [P, 2, T], F32) for s in range(2)]
+        gate = [[tile("gate%d_%d" % (s, j), [P, HALF], F32) for j in range(PACK)] for s in range(2)]
+        h = [tile("h%d" % s, [P, PACK, HALF], F32) for s in range(2)]
+        h_bf = [tile("h_bf%d" % s, [P, PACK * HALF], BF16) for s in range(2)]
+        h_codes = [tile("h_codes%d" % s, [P, HALF], U32) for s in range(2)]
+        h_scale = tile("h_scale", [P, T], U8)
+        y = [tile("y%d" % s, [P, PACK, HALF], F32) for s in range(2)]
+        warm = tile("warm", [P, 2], F32)
+
+        def cols(s):
+            return slice(s * HALF, (s + 1) * HALF)
+
+        def load_scales(plane, scales):
+            for q in range(QUADS):
+                nc.sync.dma_start(
+                    out=plane[32 * q : 32 * q + 4, :].bitcast(I32), in_=scales[0, 4 * q : 4 * q + 4, :].bitcast(I32)
+                )
+
+        nc.vector.memset(wg_scale_raw[:].bitcast(I32), 0)
+        nc.gpsimd.memset(warm[:, 0:1], 0.0)
+        nc.gpsimd.memset(v4_scale[:].bitcast(I32), 0)
+        nc.gpsimd.memset(v8_scale[:].bitcast(I32), 0)
+        nc.scalar.activation(out=warm[:, 1:2], in_=warm[:, 0:1], func=SIGMOID)
+
+        nc.sync.dma_start(out=wg_raw[:], in_=wg_words[0].rearrange("p r i -> p (r i)").bitcast(I32))
+        load_scales(wg_scale_raw, wg_scales)
+        nc.sync.dma_start(out=x_raw[0][:], in_=x_rows[:, :, cols(0)])
+        nc.sync.dma_start(out=wu_raw[:], in_=wu.rearrange("(p j) r -> p j r", j=PACK))
+        nc.sync.dma_start(out=x_raw[1][:], in_=x_rows[:, :, cols(1)])
+        load_scales(v4_scale, v4_scales)
+        nc.sync.dma_start(out=v4_codes[:].bitcast(I32), in_=v4_words[0].bitcast(I32))
+        nc.sync.dma_start(out=v8_codes[:].bitcast(I32), in_=v8_words[0].rearrange("p n i -> p (n i)").bitcast(I32))
+        nc.sync.dma_start(out=g_sb[0][:], in_=g_rows[:, 0:2, :])
+        load_scales(v8_scale, v8_scales)
+        nc.sync.dma_start(out=g_sb[1][:], in_=g_rows[:, 2:4, :])
+
+        def interleave(copy, dst, src, a, b):
+            copy(
+                out=dst[:, PACK * a : PACK * b].rearrange("p (c i j) -> p c j i", i=4, j=PACK),
+                in_=src[:, :, a:b].rearrange("p j (c i) -> p c j i", i=4),
+            )
+
+        def quantize(codes, scale, src):
+            nc.vector.quantize_mx(out=codes.bitcast(FP8X4), scales=scale, in_=src)
+
+        def deal_wu(copy, a, b):
+            copy(
+                out=wu_bf[:].rearrange("p (u m j) -> p m j u", u=PACK, j=PACK)[:, a:b],
+                in_=wu_raw[:].rearrange("p j (m u) -> p m j u", u=PACK)[:, a:b],
+            )
+
+        def first_layer(codes, scale, s, j, index, name):
+            acc = bank(index, name)
+            m = slice(j * P, (j + 1) * P)
+            nc.tensor.matmul_mx(
+                out=acc[:],
+                lhsT=codes[:, m].bitcast(FP8X4),
+                lhsT_scale=scale[:, m],
+                rhs=x_codes[s][:].bitcast(FP8X4),
+                rhs_scale=x_scale[s][:],
+                start=True,
+                stop=True,
+            )
+            return acc
+
+        def last_layer(s, c, index):
+            acc = bank(index, "y_acc%d_%d" % (s, c))
+            m = slice(c * P, (c + 1) * P)
+            nc.tensor.matmul_mx(
+                out=acc[:],
+                lhsT=v4_codes[:, 2 * c * P : 2 * (c + 1) * P].bitcast(FP4X4),
+                lhsT_scale=v4_scale[:, m],
+                rhs=h_codes[s][:].bitcast(FP8X4),
+                rhs_scale=h_scale[:, cols(s)],
+                start=True,
+                stop=False,
+            )
+            nc.tensor.matmul_mx(
+                out=acc[:],
+                lhsT=v8_codes[:, m].bitcast(FP8X4),
+                lhsT_scale=v8_scale[:, m],
+                rhs=h_codes[s][:].bitcast(FP8X4),
+                rhs_scale=h_scale[:, cols(s)],
+                start=False,
+                stop=True,
+            )
+            return acc
+
+        def gated(s, c, acc):
+            nc.vector.tensor_tensor(out=y[s][:, c, :], in0=acc[:], in1=g_sb[c // 2][:, c % 2, cols(s)], op=MULT)
+
+        nc.vector.tensor_copy(
+            out=wg_codes[:].rearrange("p (u m) -> p u m", u=PACK), in_=wg_raw[:].rearrange("p (m u) -> p u m", u=PACK)
+        )
+        nc.vector.tensor_copy(
+            out=wg_scale[:].rearrange("p (u m) -> p u m", u=PACK),
+            in_=wg_scale_raw[:].rearrange("p (m u) -> p u m", u=PACK),
+        )
+
+        interleave(nc.vector.tensor_copy, x_bf[0], x_raw[0], 0, X0_VECTOR)
+        interleave(nc.scalar.copy, x_bf[0], x_raw[0], X0_VECTOR, HALF)
+        quantize(x_codes[0][:], x_scale[0][:], x_bf[0][:])
+        ga = [first_layer(wg_codes, wg_scale, 0, j, j, "ga0_%d" % j) for j in range(PACK)]
+
+        deal_wu(nc.vector.tensor_copy, 0, WU_VECTOR)
+        deal_wu(nc.scalar.copy, WU_VECTOR, P)
+        for i in range(2):
+            quantize(wu_codes[:, 256 * i : 256 * (i + 1)], wu_scale[:, 256 * i : 256 * (i + 1)], wu_bf[:, 1024 * i : 1024 * (i + 1)])
+        ub = [first_layer(wu_codes, wu_scale, 0, j, PACK + j, "ub0_%d" % j) for j in range(PACK)]
+        for j in range(PACK):
+            nc.scalar.activation(out=gate[0][j][:], in_=ga[j][:], func=SIGMOID)
+            nc.vector.tensor_tensor(out=h[0][:, j, :], in0=ub[j][:], in1=gate[0][j][:], op=MULT)
+            if j % 2 == 1:
+                nc.sync.dma_start(out=h_rows[:, j - 1 : j + 1, cols(0)], in_=h[0][:, j - 1 : j + 1, :])
+
+        interleave(nc.scalar.copy, x_bf[1], x_raw[1], 0, X1_SCALAR)
+        interleave(nc.vector.tensor_copy, x_bf[1], x_raw[1], X1_SCALAR, HALF)
+        quantize(x_codes[1][:], x_scale[1][:], x_bf[1][:])
+        interleave(nc.scalar.copy, h_bf[0], h[0], 0, H0_SCALAR)
+        interleave(nc.vector.tensor_copy, h_bf[0], h[0], H0_SCALAR, HALF)
+        quantize(h_codes[0][:], h_scale[:, cols(0)], h_bf[0][:])
+        nc.sync.dma_start(out=code_rows[:, cols(0)], in_=h_codes[0][:].bitcast(I32))
+
+        for j in range(PACK):
+            ga_j = first_layer(wg_codes, wg_scale, 1, j, j, "ga1_%d" % j)
+            ub_j = first_layer(wu_codes, wu_scale, 1, j, PACK + j, "ub1_%d" % j)
+            nc.scalar.activation(out=gate[1][j][:], in_=ga_j[:], func=SIGMOID)
+            nc.vector.tensor_tensor(out=h[1][:, j, :], in0=ub_j[:], in1=gate[1][j][:], op=MULT)
+            if j % 2 == 1:
+                nc.sync.dma_start(out=h_rows[:, j - 1 : j + 1, cols(1)], in_=h[1][:, j - 1 : j + 1, :])
+
+        interleave(nc.scalar.copy, h_bf[1], h[1], 0, HALF)
+        for c in range(PACK):
+            gated(0, c, last_layer(0, c, c))
+            if c % 2 == 1:
+                nc.sync.dma_start(out=y_rows[:, c - 1 : c + 1, cols(0)], in_=y[0][:, c - 1 : c + 1, :])
+
+        quantize(h_codes[1][:], h_scale[:, cols(1)], h_bf[1][:])
+        nc.sync.dma_start(out=code_rows[:, cols(1)], in_=h_codes[1][:].bitcast(I32))
+        for q in range(QUADS):
+            nc.sync.dma_start(
+                out=out_3[0, 4 * q : 4 * q + 4, :].bitcast(I32), in_=h_scale[32 * q : 32 * q + 4, :].bitcast(I32)
+            )
+        for c in range(PACK):
+            gated(1, c, last_layer(1, c, PACK + c))
+            nc.sync.dma_start(out=y_rows[:, c, cols(1)], in_=y[1][:, c, :])

@@ -20,10 +20,15 @@ PACK = 4
 HALF = T // 2
 QUADS = 4
 
-X0_VECTOR = 320
-WU_VECTOR = 80
-X1_SCALAR = 384
-H0_SCALAR = 256
+CHUNK = T // 4
+PIECE = CHUNK // 2
+BANKS = 8
+ADD = mybir.AluOpType.add
+
+X_SCALAR = 192
+WU_VECTOR = 88
+WG_ROW = 8
+V8_ROW = 4
 
 
 def tile_mix_glusave_sigm_res_mul_kernel(
@@ -38,8 +43,12 @@ def tile_mix_glusave_sigm_res_mul_kernel(
         def tile(name, shape, dtype):
             return sb.tile(shape, dtype, name=name, align_bytes=64)
 
-        def bank(index, name):
-            return ps.tile([P, HALF], F32, name=name, tag="bank%d" % index)
+        taken = []
+
+        def bank():
+            n = len(taken)
+            taken.append(n)
+            return ps.tile([P, HALF], F32, name="acc%d" % n, tag="bank%d" % (n % BANKS))
 
         x_rows = x.rearrange("(p j) t -> p j t", j=PACK)
         h_rows = out_1.rearrange("(p j) t -> p j t", j=PACK)
@@ -57,14 +66,13 @@ def tile_mix_glusave_sigm_res_mul_kernel(
         wu_scale = tile("wu_scale", [P, R], U8)
         v4_codes = tile("v4_codes", [P, 2 * N], U8)
         v8_codes = tile("v8_codes", [P, N], U32)
-        v4_scale = tile("v4_scale", [P, N], U8)
-        v8_scale = tile("v8_scale", [P, N], U8)
+        v_scale = tile("v_scale", [P, N], U8)
         x_raw = [tile("x_raw%d" % s, [P, PACK, HALF], F32) for s in range(2)]
         x_bf = [tile("x_bf%d" % s, [P, PACK * HALF], BF16) for s in range(2)]
         x_codes = [tile("x_codes%d" % s, [P, HALF], U32) for s in range(2)]
         x_scale = [tile("x_scale%d" % s, [P, HALF], U8) for s in range(2)]
         g_sb = [tile("g_sb%d" % s, [P, 2, T], F32) for s in range(2)]
-        gate = [[tile("gate%d_%d" % (s, j), [P, HALF], F32) for j in range(PACK)] for s in range(2)]
+        gate = [[tile("gate%d_%d" % (q, b), [P, HALF], F32) for b in range(2)] for q in range(4)]
         h = [tile("h%d" % s, [P, PACK, HALF], F32) for s in range(2)]
         h_bf = [tile("h_bf%d" % s, [P, PACK * HALF], BF16) for s in range(2)]
         h_codes = [tile("h_codes%d" % s, [P, HALF], U32) for s in range(2)]
@@ -75,28 +83,28 @@ def tile_mix_glusave_sigm_res_mul_kernel(
         def cols(s):
             return slice(s * HALF, (s + 1) * HALF)
 
-        def load_scales(plane, scales):
-            for q in range(QUADS):
+        def load_scales(plane, row, scales):
+            for quad in range(QUADS):
                 nc.sync.dma_start(
-                    out=plane[32 * q : 32 * q + 4, :].bitcast(I32), in_=scales[0, 4 * q : 4 * q + 4, :].bitcast(I32)
+                    out=plane[32 * quad + row : 32 * quad + row + 4, :].bitcast(I32),
+                    in_=scales[0, 4 * quad : 4 * quad + 4, :].bitcast(I32),
                 )
 
         nc.vector.memset(wg_scale_raw[:].bitcast(I32), 0)
         nc.gpsimd.memset(warm[:, 0:1], 0.0)
-        nc.gpsimd.memset(v4_scale[:].bitcast(I32), 0)
-        nc.gpsimd.memset(v8_scale[:].bitcast(I32), 0)
+        nc.gpsimd.memset(v_scale[:].bitcast(I32), 0)
         nc.scalar.activation(out=warm[:, 1:2], in_=warm[:, 0:1], func=SIGMOID)
 
         nc.sync.dma_start(out=wg_raw[:], in_=wg_words[0].rearrange("p r i -> p (r i)").bitcast(I32))
-        load_scales(wg_scale_raw, wg_scales)
+        load_scales(wg_scale_raw, WG_ROW, wg_scales)
         nc.sync.dma_start(out=x_raw[0][:], in_=x_rows[:, :, cols(0)])
         nc.sync.dma_start(out=wu_raw[:], in_=wu.rearrange("(p j) r -> p j r", j=PACK))
         nc.sync.dma_start(out=x_raw[1][:], in_=x_rows[:, :, cols(1)])
-        load_scales(v4_scale, v4_scales)
+        load_scales(v_scale, 0, v4_scales)
         nc.sync.dma_start(out=v4_codes[:].bitcast(I32), in_=v4_words[0].bitcast(I32))
         nc.sync.dma_start(out=v8_codes[:].bitcast(I32), in_=v8_words[0].rearrange("p n i -> p (n i)").bitcast(I32))
         nc.sync.dma_start(out=g_sb[0][:], in_=g_rows[:, 0:2, :])
-        load_scales(v8_scale, v8_scales)
+        load_scales(v_scale, V8_ROW, v8_scales)
         nc.sync.dma_start(out=g_sb[1][:], in_=g_rows[:, 2:4, :])
 
         def interleave(copy, dst, src, a, b):
@@ -114,27 +122,71 @@ def tile_mix_glusave_sigm_res_mul_kernel(
                 in_=wu_raw[:].rearrange("p j (m u) -> p m j u", u=PACK)[:, a:b],
             )
 
-        def first_layer(codes, scale, s, j, index, name):
-            acc = bank(index, name)
-            m = slice(j * P, (j + 1) * P)
-            nc.tensor.matmul_mx(
-                out=acc[:],
-                lhsT=codes[:, m].bitcast(FP8X4),
-                lhsT_scale=scale[:, m],
-                rhs=x_codes[s][:].bitcast(FP8X4),
-                rhs_scale=x_scale[s][:],
-                start=True,
-                stop=True,
-            )
+        def first_layer(codes, scale, row, q, b):
+            acc = bank()
+            t = slice((q % 2) * CHUNK, (q % 2 + 1) * CHUNK)
+            for i in range(2):
+                m = slice((2 * b + i) * P, (2 * b + i + 1) * P)
+                nc.tensor.matmul_mx(
+                    out=acc[:, i * CHUNK : (i + 1) * CHUNK],
+                    lhsT=codes[:, m].bitcast(FP8X4),
+                    lhsT_scale=scale[row:P, m],
+                    rhs=x_codes[q // 2][:, t].bitcast(FP8X4),
+                    rhs_scale=x_scale[q // 2][:, t],
+                    start=True,
+                    stop=True,
+                )
             return acc
 
-        def last_layer(s, c, index):
-            acc = bank(index, "y_acc%d_%d" % (s, c))
+        def gate_sums(q, b):
+            return first_layer(wg_codes, wg_scale, WG_ROW, q, b)
+
+        def up_sums(q, b):
+            return first_layer(wu_codes, wu_scale, 0, q, b)
+
+        def sigmoid(q, b, acc):
+            nc.scalar.activation(out=gate[q][b][:], in_=acc[:], func=SIGMOID)
+
+        def hidden(q, b, acc):
+            o = (q % 2) * CHUNK
+            nc.vector.tensor_tensor(
+                out=h[q // 2][:, 2 * b : 2 * b + 2, o : o + CHUNK],
+                in0=acc[:].rearrange("p (j t) -> p j t", j=2),
+                in1=gate[q][b][:].rearrange("p (j t) -> p j t", j=2),
+                op=MULT,
+            )
+            if q % 2 == 1:
+                nc.sync.dma_start(out=h_rows[:, 2 * b : 2 * b + 2, cols(q // 2)], in_=h[q // 2][:, 2 * b : 2 * b + 2, :])
+
+        def round_h_scalar(q):
+            o = (q % 2) * CHUNK
+            interleave(nc.scalar.copy, h_bf[q // 2], h[q // 2], o, o + PIECE)
+
+        def round_h_gpsimd(q):
+            o = (q % 2) * CHUNK + PIECE
+            nc.gpsimd.tensor_scalar(
+                out=h_bf[q // 2][:, PACK * o : PACK * (o + PIECE)].rearrange("p (c j) -> p c j", j=PACK),
+                in0=h[q // 2][:, :, o : o + PIECE].rearrange("p j c -> p c j"),
+                scalar1=1.0,
+                scalar2=-0.0,
+                op0=MULT,
+                op1=ADD,
+            )
+
+        def quantize_x(q):
+            o = (q % 2) * CHUNK
+            quantize(x_codes[q // 2][:, o : o + CHUNK], x_scale[q // 2][:, o : o + CHUNK], x_bf[q // 2][:, PACK * o : PACK * (o + CHUNK)])
+
+        def quantize_h(s, a, b):
+            quantize(h_codes[s][:, a:b], h_scale[:, s * HALF + a : s * HALF + b], h_bf[s][:, PACK * a : PACK * b])
+
+        def last_layer(s, c):
+            acc = bank()
             m = slice(c * P, (c + 1) * P)
             nc.tensor.matmul_mx(
                 out=acc[:],
                 lhsT=v4_codes[:, 2 * c * P : 2 * (c + 1) * P].bitcast(FP4X4),
-                lhsT_scale=v4_scale[:, m],
+                lhsT_scale=v_scale[:, m],
                 rhs=h_codes[s][:].bitcast(FP8X4),
                 rhs_scale=h_scale[:, cols(s)],
                 start=True,
@@ -143,7 +195,7 @@ def tile_mix_glusave_sigm_res_mul_kernel(
             nc.tensor.matmul_mx(
                 out=acc[:],
                 lhsT=v8_codes[:, m].bitcast(FP8X4),
-                lhsT_scale=v8_scale[:, m],
+                lhsT_scale=v_scale[V8_ROW:P, m],
                 rhs=h_codes[s][:].bitcast(FP8X4),
                 rhs_scale=h_scale[:, cols(s)],
                 start=False,
@@ -153,6 +205,8 @@ def tile_mix_glusave_sigm_res_mul_kernel(
 
         def gated(s, c, acc):
             nc.vector.tensor_tensor(out=y[s][:, c, :], in0=acc[:], in1=g_sb[c // 2][:, c % 2, cols(s)], op=MULT)
+            if c % 2 == 1:
+                nc.sync.dma_start(out=y_rows[:, c - 1 : c + 1, cols(s)], in_=y[s][:, c - 1 : c + 1, :])
 
         nc.vector.tensor_copy(
             out=wg_codes[:].rearrange("p (u m) -> p u m", u=PACK), in_=wg_raw[:].rearrange("p (m u) -> p u m", u=PACK)
@@ -162,50 +216,55 @@ def tile_mix_glusave_sigm_res_mul_kernel(
             in_=wg_scale_raw[:].rearrange("p (m u) -> p u m", u=PACK),
         )
 
-        interleave(nc.vector.tensor_copy, x_bf[0], x_raw[0], 0, X0_VECTOR)
-        interleave(nc.scalar.copy, x_bf[0], x_raw[0], X0_VECTOR, HALF)
-        quantize(x_codes[0][:], x_scale[0][:], x_bf[0][:])
-        ga = [first_layer(wg_codes, wg_scale, 0, j, j, "ga0_%d" % j) for j in range(PACK)]
+        interleave(nc.vector.tensor_copy, x_bf[0], x_raw[0], 0, CHUNK)
+        interleave(nc.scalar.copy, x_bf[0], x_raw[0], CHUNK, CHUNK + X_SCALAR)
+        interleave(nc.vector.tensor_copy, x_bf[0], x_raw[0], CHUNK + X_SCALAR, HALF)
+        quantize_x(0)
+        quantize_x(1)
+        ga = [gate_sums(0, b) for b in range(2)]
 
         deal_wu(nc.vector.tensor_copy, 0, WU_VECTOR)
         deal_wu(nc.scalar.copy, WU_VECTOR, P)
-        for i in range(2):
-            quantize(wu_codes[:, 256 * i : 256 * (i + 1)], wu_scale[:, 256 * i : 256 * (i + 1)], wu_bf[:, 1024 * i : 1024 * (i + 1)])
-        ub = [first_layer(wu_codes, wu_scale, 0, j, PACK + j, "ub0_%d" % j) for j in range(PACK)]
-        for j in range(PACK):
-            nc.scalar.activation(out=gate[0][j][:], in_=ga[j][:], func=SIGMOID)
-            nc.vector.tensor_tensor(out=h[0][:, j, :], in0=ub[j][:], in1=gate[0][j][:], op=MULT)
-            if j % 2 == 1:
-                nc.sync.dma_start(out=h_rows[:, j - 1 : j + 1, cols(0)], in_=h[0][:, j - 1 : j + 1, :])
+        for b in range(2):
+            quantize(wu_codes[:, 256 * b : 256 * (b + 1)], wu_scale[:, 256 * b : 256 * (b + 1)], wu_bf[:, 1024 * b : 1024 * (b + 1)])
+        ub = [up_sums(0, b) for b in range(2)]
+        for b in range(2):
+            sigmoid(0, b, ga[b])
 
-        interleave(nc.scalar.copy, x_bf[1], x_raw[1], 0, X1_SCALAR)
-        interleave(nc.vector.tensor_copy, x_bf[1], x_raw[1], X1_SCALAR, HALF)
-        quantize(x_codes[1][:], x_scale[1][:], x_bf[1][:])
-        interleave(nc.scalar.copy, h_bf[0], h[0], 0, H0_SCALAR)
-        interleave(nc.vector.tensor_copy, h_bf[0], h[0], H0_SCALAR, HALF)
-        quantize(h_codes[0][:], h_scale[:, cols(0)], h_bf[0][:])
-        nc.sync.dma_start(out=code_rows[:, cols(0)], in_=h_codes[0][:].bitcast(I32))
+        interleave(nc.vector.tensor_copy, x_bf[1], x_raw[1], 0, PIECE)
+        interleave(nc.vector.tensor_copy, x_bf[1], x_raw[1], HALF - PIECE, HALF)
+        interleave(nc.scalar.copy, x_bf[1], x_raw[1], PIECE, CHUNK)
+        interleave(nc.scalar.copy, x_bf[1], x_raw[1], CHUNK, HALF - PIECE)
+        for b in range(2):
+            hidden(0, b, ub[b])
+        round_h_gpsimd(0)
+        quantize_x(2)
 
-        for j in range(PACK):
-            ga_j = first_layer(wg_codes, wg_scale, 1, j, j, "ga1_%d" % j)
-            ub_j = first_layer(wu_codes, wu_scale, 1, j, PACK + j, "ub1_%d" % j)
-            nc.scalar.activation(out=gate[1][j][:], in_=ga_j[:], func=SIGMOID)
-            nc.vector.tensor_tensor(out=h[1][:, j, :], in0=ub_j[:], in1=gate[1][j][:], op=MULT)
-            if j % 2 == 1:
-                nc.sync.dma_start(out=h_rows[:, j - 1 : j + 1, cols(1)], in_=h[1][:, j - 1 : j + 1, :])
+        for q in range(1, 4):
+            for b in range(2):
+                ga_b = gate_sums(q, b)
+                ub_b = up_sums(q, b)
+                sigmoid(q, b, ga_b)
+                hidden(q, b, ub_b)
+                if q == 1 and b == 0:
+                    quantize_x(3)
+            round_h_scalar(q - 1)
+            round_h_gpsimd(q)
+            if q == 2:
+                quantize_h(0, 0, HALF)
+                nc.sync.dma_start(out=code_rows[:, cols(0)], in_=h_codes[0][:].bitcast(I32))
+        round_h_scalar(3)
+        quantize_h(1, 0, CHUNK)
 
-        interleave(nc.scalar.copy, h_bf[1], h[1], 0, HALF)
         for c in range(PACK):
-            gated(0, c, last_layer(0, c, c))
-            if c % 2 == 1:
-                nc.sync.dma_start(out=y_rows[:, c - 1 : c + 1, cols(0)], in_=y[0][:, c - 1 : c + 1, :])
-
-        quantize(h_codes[1][:], h_scale[:, cols(1)], h_bf[1][:])
-        nc.sync.dma_start(out=code_rows[:, cols(1)], in_=h_codes[1][:].bitcast(I32))
-        for q in range(QUADS):
-            nc.sync.dma_start(
-                out=out_3[0, 4 * q : 4 * q + 4, :].bitcast(I32), in_=h_scale[32 * q : 32 * q + 4, :].bitcast(I32)
-            )
+            gated(0, c, last_layer(0, c))
+            if c == 1:
+                quantize_h(1, CHUNK, HALF)
+                nc.sync.dma_start(out=code_rows[:, cols(1)], in_=h_codes[1][:].bitcast(I32))
+                for quad in range(QUADS):
+                    nc.sync.dma_start(
+                        out=out_3[0, 4 * quad : 4 * quad + 4, :].bitcast(I32),
+                        in_=h_scale[32 * quad : 32 * quad + 4, :].bitcast(I32),
+                    )
         for c in range(PACK):
-            gated(1, c, last_layer(1, c, PACK + c))
-            nc.sync.dma_start(out=y_rows[:, c, cols(1)], in_=y[1][:, c, :])
+            gated(1, c, last_layer(1, c))

@@ -71,7 +71,7 @@ def tile_mix_glusave_sigm_res_mul_kernel(
         x_bf = [tile("x_bf%d" % s, [P, PACK * HALF], BF16) for s in range(2)]
         x_codes = [tile("x_codes%d" % s, [P, HALF], U32) for s in range(2)]
         x_scale = [tile("x_scale%d" % s, [P, HALF], U8) for s in range(2)]
-        g_sb = [tile("g_sb%d" % s, [P, 2, T], F32) for s in range(2)]
+        g_sb = tile("g_sb", [P, PACK, T], F32)
         gate = [[tile("gate%d_%d" % (q, b), [P, HALF], F32) for b in range(2)] for q in range(4)]
         h = [tile("h%d" % s, [P, PACK, HALF], F32) for s in range(2)]
         h_bf = [tile("h_bf%d" % s, [P, PACK * HALF], BF16) for s in range(2)]
@@ -83,9 +83,9 @@ def tile_mix_glusave_sigm_res_mul_kernel(
         def cols(s):
             return slice(s * HALF, (s + 1) * HALF)
 
-        def load_scales(plane, row, scales):
+        def load_scales(engine, plane, row, scales):
             for quad in range(QUADS):
-                nc.sync.dma_start(
+                engine.dma_start(
                     out=plane[32 * quad + row : 32 * quad + row + 4, :].bitcast(I32),
                     in_=scales[0, 4 * quad : 4 * quad + 4, :].bitcast(I32),
                 )
@@ -93,19 +93,18 @@ def tile_mix_glusave_sigm_res_mul_kernel(
         nc.vector.memset(wg_scale_raw[:].bitcast(I32), 0)
         nc.gpsimd.memset(warm[:, 0:1], 0.0)
         nc.gpsimd.memset(v_scale[:].bitcast(I32), 0)
-        nc.scalar.activation(out=warm[:, 1:2], in_=warm[:, 0:1], func=SIGMOID)
 
-        nc.sync.dma_start(out=wg_raw[:], in_=wg_words[0].rearrange("p r i -> p (r i)").bitcast(I32))
-        load_scales(wg_scale_raw, WG_ROW, wg_scales)
+        nc.scalar.activation(out=warm[:, 1:2], in_=warm[:, 0:1], func=SIGMOID)
         nc.sync.dma_start(out=x_raw[0][:], in_=x_rows[:, :, cols(0)])
+        load_scales(nc.sync, wg_scale_raw, WG_ROW, wg_scales)
+        nc.sync.dma_start(out=wg_raw[:], in_=wg_words[0].rearrange("p r i -> p (r i)").bitcast(I32))
         nc.sync.dma_start(out=wu_raw[:], in_=wu.rearrange("(p j) r -> p j r", j=PACK))
         nc.sync.dma_start(out=x_raw[1][:], in_=x_rows[:, :, cols(1)])
-        load_scales(v_scale, 0, v4_scales)
+        load_scales(nc.gpsimd, v_scale, 0, v4_scales)
+        load_scales(nc.gpsimd, v_scale, V8_ROW, v8_scales)
         nc.sync.dma_start(out=v4_codes[:].bitcast(I32), in_=v4_words[0].bitcast(I32))
         nc.sync.dma_start(out=v8_codes[:].bitcast(I32), in_=v8_words[0].rearrange("p n i -> p (n i)").bitcast(I32))
-        nc.sync.dma_start(out=g_sb[0][:], in_=g_rows[:, 0:2, :])
-        load_scales(v_scale, V8_ROW, v8_scales)
-        nc.sync.dma_start(out=g_sb[1][:], in_=g_rows[:, 2:4, :])
+        nc.sync.dma_start(out=g_sb[:], in_=g_rows)
 
         def interleave(copy, dst, src, a, b):
             copy(
@@ -204,21 +203,21 @@ def tile_mix_glusave_sigm_res_mul_kernel(
             return acc
 
         def gated(s, c, acc):
-            nc.vector.tensor_tensor(out=y[s][:, c, :], in0=acc[:], in1=g_sb[c // 2][:, c % 2, cols(s)], op=MULT)
+            nc.vector.tensor_tensor(out=y[s][:, c, :], in0=acc[:], in1=g_sb[:, c, cols(s)], op=MULT)
             if c % 2 == 1:
                 nc.sync.dma_start(out=y_rows[:, c - 1 : c + 1, cols(s)], in_=y[s][:, c - 1 : c + 1, :])
 
-        nc.vector.tensor_copy(
-            out=wg_codes[:].rearrange("p (u m) -> p u m", u=PACK), in_=wg_raw[:].rearrange("p (m u) -> p u m", u=PACK)
-        )
+        interleave(nc.vector.tensor_copy, x_bf[0], x_raw[0], 0, CHUNK)
+        interleave(nc.scalar.copy, x_bf[0], x_raw[0], CHUNK, CHUNK + X_SCALAR)
+        interleave(nc.vector.tensor_copy, x_bf[0], x_raw[0], CHUNK + X_SCALAR, HALF)
         nc.vector.tensor_copy(
             out=wg_scale[:].rearrange("p (u m) -> p u m", u=PACK),
             in_=wg_scale_raw[:].rearrange("p (m u) -> p u m", u=PACK),
         )
 
-        interleave(nc.vector.tensor_copy, x_bf[0], x_raw[0], 0, CHUNK)
-        interleave(nc.scalar.copy, x_bf[0], x_raw[0], CHUNK, CHUNK + X_SCALAR)
-        interleave(nc.vector.tensor_copy, x_bf[0], x_raw[0], CHUNK + X_SCALAR, HALF)
+        nc.vector.tensor_copy(
+            out=wg_codes[:].rearrange("p (u m) -> p u m", u=PACK), in_=wg_raw[:].rearrange("p (m u) -> p u m", u=PACK)
+        )
         quantize_x(0)
         quantize_x(1)
         ga = [gate_sums(0, b) for b in range(2)]
@@ -250,8 +249,10 @@ def tile_mix_glusave_sigm_res_mul_kernel(
                     quantize_x(3)
             round_h_scalar(q - 1)
             round_h_gpsimd(q)
+            if q == 1:
+                quantize_h(0, 0, CHUNK)
             if q == 2:
-                quantize_h(0, 0, HALF)
+                quantize_h(0, CHUNK, HALF)
                 nc.sync.dma_start(out=code_rows[:, cols(0)], in_=h_codes[0][:].bitcast(I32))
         round_h_scalar(3)
         quantize_h(1, 0, CHUNK)
@@ -262,7 +263,7 @@ def tile_mix_glusave_sigm_res_mul_kernel(
                 quantize_h(1, CHUNK, HALF)
                 nc.sync.dma_start(out=code_rows[:, cols(1)], in_=h_codes[1][:].bitcast(I32))
                 for quad in range(QUADS):
-                    nc.sync.dma_start(
+                    nc.gpsimd.dma_start(
                         out=out_3[0, 4 * quad : 4 * quad + 4, :].bitcast(I32),
                         in_=h_scale[32 * quad : 32 * quad + 4, :].bitcast(I32),
                     )

@@ -14,21 +14,22 @@ FP8X4 = mybir.dt.float8_e4m3fn_x4
 FP4X4 = mybir.dt.float4_e2m1fn_x4
 SIGMOID = mybir.ActivationFunctionType.Sigmoid
 MULT = mybir.AluOpType.mult
+ADD = mybir.AluOpType.add
 
 P = 128
 PACK = 4
-HALF = T // 2
 QUADS = 4
-
+BANKS = 8
+HALF = T // 2
 CHUNK = T // 4
 PIECE = CHUNK // 2
-BANKS = 8
-ADD = mybir.AluOpType.add
+LINE = 4
+N_BLOCKS = N // P
 
-X_SCALAR = 192
-WU_VECTOR = 88
-WG_ROW = 8
-V8_ROW = 4
+V4_ROW, V8_ROW, WG_ROW = 0, 4, 8
+
+STEPS = [(chunk, pair) for chunk in range(4) for pair in range(2)]
+EARLY = 3
 
 
 def tile_mix_glusave_sigm_res_mul_kernel(
@@ -43,229 +44,235 @@ def tile_mix_glusave_sigm_res_mul_kernel(
         def tile(name, shape, dtype):
             return sb.tile(shape, dtype, name=name, align_bytes=64)
 
-        taken = []
+        banks_taken = []
 
-        def bank():
-            n = len(taken)
-            taken.append(n)
-            return ps.tile([P, HALF], F32, name="acc%d" % n, tag="bank%d" % (n % BANKS))
+        def next_bank():
+            count = len(banks_taken)
+            banks_taken.append(count)
+            return ps.tile([P, HALF], F32, name="acc%d" % count, tag="bank%d" % (count % BANKS))
 
         x_rows = x.rearrange("(p j) t -> p j t", j=PACK)
         h_rows = out_1.rearrange("(p j) t -> p j t", j=PACK)
         g_rows = g.rearrange("(c p) t -> p c t", p=P)
         y_rows = out_0.rearrange("(c p) t -> p c t", p=P)
-        code_rows = out_2[0].rearrange("p t i -> p (t i)").bitcast(I32)
+        h_word_rows = out_2[0].rearrange("p t i -> p (t i)").bitcast(I32)
 
         wg_raw = tile("wg_raw", [P, R], I32)
-        wg_scale_raw = tile("wg_scale_raw", [P, R], U8)
+        wg_plane_raw = tile("wg_plane_raw", [P, R], U8)
         wg_codes = tile("wg_codes", [P, R], I32)
-        wg_scale = tile("wg_scale", [P, R], U8)
+        wg_plane = tile("wg_plane", [P, R], U8)
         wu_raw = tile("wu_raw", [P, PACK, R], F32)
         wu_bf = tile("wu_bf", [P, PACK * R], BF16)
         wu_codes = tile("wu_codes", [P, R], U32)
-        wu_scale = tile("wu_scale", [P, R], U8)
+        wu_plane = tile("wu_plane", [P, R], U8)
         v4_codes = tile("v4_codes", [P, 2 * N], U8)
         v8_codes = tile("v8_codes", [P, N], U32)
-        v_scale = tile("v_scale", [P, N], U8)
-        x_raw = [tile("x_raw%d" % s, [P, PACK, HALF], F32) for s in range(2)]
-        x_bf = [tile("x_bf%d" % s, [P, PACK * HALF], BF16) for s in range(2)]
-        x_codes = [tile("x_codes%d" % s, [P, HALF], U32) for s in range(2)]
-        x_scale = [tile("x_scale%d" % s, [P, HALF], U8) for s in range(2)]
-        g_sb = tile("g_sb", [P, PACK, T], F32)
-        gate = [[tile("gate%d_%d" % (q, b), [P, HALF], F32) for b in range(2)] for q in range(4)]
-        h = [tile("h%d" % s, [P, PACK, HALF], F32) for s in range(2)]
-        h_bf = [tile("h_bf%d" % s, [P, PACK * HALF], BF16) for s in range(2)]
-        h_codes = [tile("h_codes%d" % s, [P, HALF], U32) for s in range(2)]
-        h_scale = tile("h_scale", [P, T], U8)
-        y = [tile("y%d" % s, [P, PACK, HALF], F32) for s in range(2)]
-        warm = tile("warm", [P, 2], F32)
+        v_planes = tile("v_planes", [P, N], U8)
+        x_raw = [tile("x_raw%d" % half, [P, PACK, HALF], F32) for half in range(2)]
+        x_bf = [tile("x_bf%d" % half, [P, PACK * HALF], BF16) for half in range(2)]
+        x_codes = [tile("x_codes%d" % half, [P, HALF], U32) for half in range(2)]
+        x_plane = [tile("x_plane%d" % half, [P, HALF], U8) for half in range(2)]
+        g_sb = tile("g_sb", [P, N_BLOCKS, T], F32)
+        gate = {step: tile("gate%d_%d" % step, [P, 2 * CHUNK], F32) for step in STEPS}
+        h = [tile("h%d" % half, [P, PACK, HALF], F32) for half in range(2)]
+        h_bf = [tile("h_bf%d" % half, [P, PACK * HALF], BF16) for half in range(2)]
+        h_codes = [tile("h_codes%d" % half, [P, HALF], U32) for half in range(2)]
+        h_plane = tile("h_plane", [P, T], U8)
+        y = [tile("y%d" % half, [P, N_BLOCKS, HALF], F32) for half in range(2)]
 
-        def cols(s):
-            return slice(s * HALF, (s + 1) * HALF)
+        def half_cols(half):
+            return slice(half * HALF, (half + 1) * HALF)
 
-        def load_scales(engine, plane, row, scales):
+        def place(chunk):
+            return chunk // 2, (chunk % 2) * CHUNK
+
+        def load_plane(engine, plane, row, scales):
             for quad in range(QUADS):
                 engine.dma_start(
                     out=plane[32 * quad + row : 32 * quad + row + 4, :].bitcast(I32),
                     in_=scales[0, 4 * quad : 4 * quad + 4, :].bitcast(I32),
                 )
 
-        nc.vector.memset(wg_scale_raw[:].bitcast(I32), 0)
-        nc.gpsimd.memset(warm[:, 0:1], 0.0)
-        nc.gpsimd.memset(v_scale[:].bitcast(I32), 0)
-
-        nc.scalar.activation(out=warm[:, 1:2], in_=warm[:, 0:1], func=SIGMOID)
-        nc.sync.dma_start(out=x_raw[0][:], in_=x_rows[:, :, cols(0)])
-        load_scales(nc.sync, wg_scale_raw, WG_ROW, wg_scales)
-        nc.sync.dma_start(out=wg_raw[:], in_=wg_words[0].rearrange("p r i -> p (r i)").bitcast(I32))
-        nc.sync.dma_start(out=wu_raw[:], in_=wu.rearrange("(p j) r -> p j r", j=PACK))
-        nc.sync.dma_start(out=x_raw[1][:], in_=x_rows[:, :, cols(1)])
-        load_scales(nc.gpsimd, v_scale, 0, v4_scales)
-        load_scales(nc.gpsimd, v_scale, V8_ROW, v8_scales)
-        nc.sync.dma_start(out=v4_codes[:].bitcast(I32), in_=v4_words[0].bitcast(I32))
-        nc.sync.dma_start(out=v8_codes[:].bitcast(I32), in_=v8_words[0].rearrange("p n i -> p (n i)").bitcast(I32))
-        nc.sync.dma_start(out=g_sb[:], in_=g_rows)
-
-        def interleave(copy, dst, src, a, b):
+        def interleave(copy, dst, src, first, last):
             copy(
-                out=dst[:, PACK * a : PACK * b].rearrange("p (c i j) -> p c j i", i=4, j=PACK),
-                in_=src[:, :, a:b].rearrange("p j (c i) -> p c j i", i=4),
+                out=dst[:, PACK * first : PACK * last].rearrange("p (c i j) -> p c j i", i=LINE, j=PACK),
+                in_=src[:, :, first:last].rearrange("p j (c i) -> p c j i", i=LINE),
             )
 
-        def quantize(codes, scale, src):
-            nc.vector.quantize_mx(out=codes.bitcast(FP8X4), scales=scale, in_=src)
+        def quantize(codes, plane, src):
+            nc.vector.quantize_mx(out=codes.bitcast(FP8X4), scales=plane, in_=src)
 
-        def deal_wu(copy, a, b):
-            copy(
-                out=wu_bf[:].rearrange("p (u m j) -> p m j u", u=PACK, j=PACK)[:, a:b],
-                in_=wu_raw[:].rearrange("p j (m u) -> p m j u", u=PACK)[:, a:b],
+        def quantize_x(chunk):
+            half, first = place(chunk)
+            quantize(
+                x_codes[half][:, first : first + CHUNK],
+                x_plane[half][:, first : first + CHUNK],
+                x_bf[half][:, PACK * first : PACK * (first + CHUNK)],
             )
 
-        def first_layer(codes, scale, row, q, b):
-            acc = bank()
-            t = slice((q % 2) * CHUNK, (q % 2 + 1) * CHUNK)
+        def quantize_h(chunk):
+            half, first = place(chunk)
+            quantize(
+                h_codes[half][:, first : first + CHUNK],
+                h_plane[:, chunk * CHUNK : (chunk + 1) * CHUNK],
+                h_bf[half][:, PACK * first : PACK * (first + CHUNK)],
+            )
+            if chunk % 2 == 1:
+                nc.sync.dma_start(out=h_word_rows[:, half_cols(half)], in_=h_codes[half][:].bitcast(I32))
+
+        def first_layer(codes, plane, row, step):
+            chunk, pair = step
+            half, first = place(chunk)
+            acc = next_bank()
             for i in range(2):
-                m = slice((2 * b + i) * P, (2 * b + i + 1) * P)
+                dealt = slice((2 * pair + i) * P, (2 * pair + i + 1) * P)
                 nc.tensor.matmul_mx(
                     out=acc[:, i * CHUNK : (i + 1) * CHUNK],
-                    lhsT=codes[:, m].bitcast(FP8X4),
-                    lhsT_scale=scale[row:P, m],
-                    rhs=x_codes[q // 2][:, t].bitcast(FP8X4),
-                    rhs_scale=x_scale[q // 2][:, t],
+                    lhsT=codes[:, dealt].bitcast(FP8X4),
+                    lhsT_scale=plane[row:P, dealt],
+                    rhs=x_codes[half][:, first : first + CHUNK].bitcast(FP8X4),
+                    rhs_scale=x_plane[half][:, first : first + CHUNK],
                     start=True,
                     stop=True,
                 )
             return acc
 
-        def gate_sums(q, b):
-            return first_layer(wg_codes, wg_scale, WG_ROW, q, b)
+        def gate_sums(step):
+            return first_layer(wg_codes, wg_plane, WG_ROW, step)
 
-        def up_sums(q, b):
-            return first_layer(wu_codes, wu_scale, 0, q, b)
+        def up_sums(step):
+            return first_layer(wu_codes, wu_plane, 0, step)
 
-        def sigmoid(q, b, acc):
-            nc.scalar.activation(out=gate[q][b][:], in_=acc[:], func=SIGMOID)
+        def sigmoid(step, ga):
+            nc.scalar.activation(out=gate[step][:], in_=ga[:], func=SIGMOID)
 
-        def hidden(q, b, acc):
-            o = (q % 2) * CHUNK
+        def hidden(step, ub):
+            chunk, pair = step
+            half, first = place(chunk)
+            rows = slice(2 * pair, 2 * pair + 2)
             nc.vector.tensor_tensor(
-                out=h[q // 2][:, 2 * b : 2 * b + 2, o : o + CHUNK],
-                in0=acc[:].rearrange("p (j t) -> p j t", j=2),
-                in1=gate[q][b][:].rearrange("p (j t) -> p j t", j=2),
+                out=h[half][:, rows, first : first + CHUNK],
+                in0=ub[:].rearrange("p (j t) -> p j t", j=2),
+                in1=gate[step][:].rearrange("p (j t) -> p j t", j=2),
                 op=MULT,
             )
-            if q % 2 == 1:
-                nc.sync.dma_start(out=h_rows[:, 2 * b : 2 * b + 2, cols(q // 2)], in_=h[q // 2][:, 2 * b : 2 * b + 2, :])
+            if chunk % 2 == 1:
+                nc.sync.dma_start(out=h_rows[:, rows, half_cols(half)], in_=h[half][:, rows, :])
 
-        def round_h_scalar(q):
-            o = (q % 2) * CHUNK
-            interleave(nc.scalar.copy, h_bf[q // 2], h[q // 2], o, o + PIECE)
+        def round_h_scalar(chunk):
+            half, first = place(chunk)
+            interleave(nc.scalar.copy, h_bf[half], h[half], first, first + PIECE)
 
-        def round_h_gpsimd(q):
-            o = (q % 2) * CHUNK + PIECE
+        def round_h_gpsimd(chunk):
+            half, first = place(chunk)
+            piece = slice(first + PIECE, first + CHUNK)
             nc.gpsimd.tensor_scalar(
-                out=h_bf[q // 2][:, PACK * o : PACK * (o + PIECE)].rearrange("p (c j) -> p c j", j=PACK),
-                in0=h[q // 2][:, :, o : o + PIECE].rearrange("p j c -> p c j"),
+                out=h_bf[half][:, PACK * piece.start : PACK * piece.stop].rearrange("p (c j) -> p c j", j=PACK),
+                in0=h[half][:, :, piece].rearrange("p j c -> p c j"),
                 scalar1=1.0,
                 scalar2=-0.0,
                 op0=MULT,
                 op1=ADD,
             )
 
-        def quantize_x(q):
-            o = (q % 2) * CHUNK
-            quantize(x_codes[q // 2][:, o : o + CHUNK], x_scale[q // 2][:, o : o + CHUNK], x_bf[q // 2][:, PACK * o : PACK * (o + CHUNK)])
-
-        def quantize_h(s, a, b):
-            quantize(h_codes[s][:, a:b], h_scale[:, s * HALF + a : s * HALF + b], h_bf[s][:, PACK * a : PACK * b])
-
-        def last_layer(s, c):
-            acc = bank()
-            m = slice(c * P, (c + 1) * P)
+        def last_layer(half, block):
+            acc = next_bank()
+            n_cols = slice(block * P, (block + 1) * P)
             nc.tensor.matmul_mx(
                 out=acc[:],
-                lhsT=v4_codes[:, 2 * c * P : 2 * (c + 1) * P].bitcast(FP4X4),
-                lhsT_scale=v_scale[:, m],
-                rhs=h_codes[s][:].bitcast(FP8X4),
-                rhs_scale=h_scale[:, cols(s)],
+                lhsT=v4_codes[:, 2 * n_cols.start : 2 * n_cols.stop].bitcast(FP4X4),
+                lhsT_scale=v_planes[V4_ROW:P, n_cols],
+                rhs=h_codes[half][:].bitcast(FP8X4),
+                rhs_scale=h_plane[:, half_cols(half)],
                 start=True,
                 stop=False,
             )
             nc.tensor.matmul_mx(
                 out=acc[:],
-                lhsT=v8_codes[:, m].bitcast(FP8X4),
-                lhsT_scale=v_scale[V8_ROW:P, m],
-                rhs=h_codes[s][:].bitcast(FP8X4),
-                rhs_scale=h_scale[:, cols(s)],
+                lhsT=v8_codes[:, n_cols].bitcast(FP8X4),
+                lhsT_scale=v_planes[V8_ROW:P, n_cols],
+                rhs=h_codes[half][:].bitcast(FP8X4),
+                rhs_scale=h_plane[:, half_cols(half)],
                 start=False,
                 stop=True,
             )
-            return acc
+            nc.vector.tensor_tensor(out=y[half][:, block, :], in0=acc[:], in1=g_sb[:, block, half_cols(half)], op=MULT)
 
-        def gated(s, c, acc):
-            nc.vector.tensor_tensor(out=y[s][:, c, :], in0=acc[:], in1=g_sb[:, c, cols(s)], op=MULT)
-            if c % 2 == 1:
-                nc.sync.dma_start(out=y_rows[:, c - 1 : c + 1, cols(s)], in_=y[s][:, c - 1 : c + 1, :])
+        def store_y(half, first, last):
+            nc.sync.dma_start(out=y_rows[:, first:last, half_cols(half)], in_=y[half][:, first:last, :])
+
+        nc.vector.memset(wg_plane_raw[:].bitcast(I32), 0)
+        nc.gpsimd.memset(v_planes[:].bitcast(I32), 0)
+
+        nc.sync.dma_start(out=x_raw[0][:], in_=x_rows[:, :, half_cols(0)])
+        load_plane(nc.sync, wg_plane_raw, WG_ROW, wg_scales)
+        nc.sync.dma_start(out=wg_raw[:], in_=wg_words[0].rearrange("p r i -> p (r i)").bitcast(I32))
+        nc.sync.dma_start(out=wu_raw[:], in_=wu.rearrange("(p j) r -> p j r", j=PACK))
+        nc.sync.dma_start(out=x_raw[1][:], in_=x_rows[:, :, half_cols(1)])
+        load_plane(nc.gpsimd, v_planes, V4_ROW, v4_scales)
+        load_plane(nc.gpsimd, v_planes, V8_ROW, v8_scales)
+        nc.sync.dma_start(out=v4_codes[:].bitcast(I32), in_=v4_words[0].bitcast(I32))
+        nc.sync.dma_start(out=v8_codes[:].bitcast(I32), in_=v8_words[0].rearrange("p n i -> p (n i)").bitcast(I32))
+        nc.sync.dma_start(out=g_sb[:], in_=g_rows)
 
         interleave(nc.vector.tensor_copy, x_bf[0], x_raw[0], 0, CHUNK)
-        interleave(nc.scalar.copy, x_bf[0], x_raw[0], CHUNK, CHUNK + X_SCALAR)
-        interleave(nc.vector.tensor_copy, x_bf[0], x_raw[0], CHUNK + X_SCALAR, HALF)
-        nc.vector.tensor_copy(
-            out=wg_scale[:].rearrange("p (u m) -> p u m", u=PACK),
-            in_=wg_scale_raw[:].rearrange("p (m u) -> p u m", u=PACK),
-        )
-
-        nc.vector.tensor_copy(
-            out=wg_codes[:].rearrange("p (u m) -> p u m", u=PACK), in_=wg_raw[:].rearrange("p (m u) -> p u m", u=PACK)
-        )
+        interleave(nc.scalar.copy, x_bf[0], x_raw[0], CHUNK, HALF)
+        for dealt_tile, raw_tile in ((wg_plane, wg_plane_raw), (wg_codes, wg_raw)):
+            nc.vector.tensor_copy(
+                out=dealt_tile[:].rearrange("p (j m) -> p j m", j=PACK),
+                in_=raw_tile[:].rearrange("p (m j) -> p j m", j=PACK),
+            )
         quantize_x(0)
         quantize_x(1)
-        ga = [gate_sums(0, b) for b in range(2)]
+        for step in STEPS[:EARLY]:
+            sigmoid(step, gate_sums(step))
 
-        deal_wu(nc.vector.tensor_copy, 0, WU_VECTOR)
-        deal_wu(nc.scalar.copy, WU_VECTOR, P)
-        for b in range(2):
-            quantize(wu_codes[:, 256 * b : 256 * (b + 1)], wu_scale[:, 256 * b : 256 * (b + 1)], wu_bf[:, 1024 * b : 1024 * (b + 1)])
-        ub = [up_sums(0, b) for b in range(2)]
-        for b in range(2):
-            sigmoid(0, b, ga[b])
+        nc.vector.tensor_copy(
+            out=wu_bf[:].rearrange("p (j m i) -> p m i j", j=PACK, i=PACK),
+            in_=wu_raw[:].rearrange("p i (m j) -> p m i j", j=PACK),
+        )
+        for pair in range(2):
+            cols = slice(2 * pair * P, 2 * (pair + 1) * P)
+            quantize(wu_codes[:, cols], wu_plane[:, cols], wu_bf[:, PACK * cols.start : PACK * cols.stop])
+        early_ub = [up_sums(step) for step in STEPS[:EARLY]]
 
         interleave(nc.vector.tensor_copy, x_bf[1], x_raw[1], 0, PIECE)
-        interleave(nc.vector.tensor_copy, x_bf[1], x_raw[1], HALF - PIECE, HALF)
         interleave(nc.scalar.copy, x_bf[1], x_raw[1], PIECE, CHUNK)
-        interleave(nc.scalar.copy, x_bf[1], x_raw[1], CHUNK, HALF - PIECE)
-        for b in range(2):
-            hidden(0, b, ub[b])
+        interleave(nc.scalar.copy, x_bf[1], x_raw[1], CHUNK, HALF)
+        hidden(STEPS[0], early_ub[0])
+        hidden(STEPS[1], early_ub[1])
         round_h_gpsimd(0)
         quantize_x(2)
+        hidden(STEPS[2], early_ub[2])
+        quantize_x(3)
 
-        for q in range(1, 4):
-            for b in range(2):
-                ga_b = gate_sums(q, b)
-                ub_b = up_sums(q, b)
-                sigmoid(q, b, ga_b)
-                hidden(q, b, ub_b)
-                if q == 1 and b == 0:
-                    quantize_x(3)
-            round_h_scalar(q - 1)
-            round_h_gpsimd(q)
-            if q == 1:
-                quantize_h(0, 0, CHUNK)
-            if q == 2:
-                quantize_h(0, CHUNK, HALF)
-                nc.sync.dma_start(out=code_rows[:, cols(0)], in_=h_codes[0][:].bitcast(I32))
+        for step in STEPS[EARLY:]:
+            chunk, pair = step
+            ga = gate_sums(step)
+            ub = up_sums(step)
+            sigmoid(step, ga)
+            hidden(step, ub)
+            if pair == 1:
+                round_h_scalar(chunk - 1)
+                round_h_gpsimd(chunk)
+                quantize_h(chunk - 1)
         round_h_scalar(3)
-        quantize_h(1, 0, CHUNK)
 
-        for c in range(PACK):
-            gated(0, c, last_layer(0, c))
-            if c == 1:
-                quantize_h(1, CHUNK, HALF)
-                nc.sync.dma_start(out=code_rows[:, cols(1)], in_=h_codes[1][:].bitcast(I32))
-                for quad in range(QUADS):
-                    nc.gpsimd.dma_start(
-                        out=out_3[0, 4 * quad : 4 * quad + 4, :].bitcast(I32),
-                        in_=h_scale[32 * quad : 32 * quad + 4, :].bitcast(I32),
-                    )
-        for c in range(PACK):
-            gated(1, c, last_layer(1, c))
+        last_layer(0, 0)
+        last_layer(0, 1)
+        store_y(0, 0, 2)
+        quantize_h(3)
+        for quad in range(QUADS):
+            nc.gpsimd.dma_start(
+                out=out_3[0, 4 * quad : 4 * quad + 4, :].bitcast(I32),
+                in_=h_plane[32 * quad : 32 * quad + 4, :].bitcast(I32),
+            )
+        last_layer(0, 2)
+        last_layer(0, 3)
+        store_y(0, 2, 4)
+        last_layer(1, 0)
+        last_layer(1, 1)
+        store_y(1, 0, 2)
+        for block in range(2, N_BLOCKS):
+            last_layer(1, block)
+            store_y(1, block, block + 1)

@@ -25,6 +25,7 @@ CHUNK = T // 4
 PIECE = CHUNK // 2
 LINE = 4
 N_BLOCKS = N // P
+ALIGN = 256
 
 V4_ROW, V8_ROW, WG_ROW = 0, 4, 8
 
@@ -42,7 +43,7 @@ def tile_mix_glusave_sigm_res_mul_kernel(
         ctx.enter_context(tc.manual_schedule())
 
         def tile(name, shape, dtype):
-            return sb.tile(shape, dtype, name=name, align_bytes=64)
+            return sb.tile(shape, dtype, name=name, align_bytes=ALIGN)
 
         banks_taken = []
 
@@ -263,7 +264,7 @@ def tile_mix_glusave_sigm_res_mul_kernel(
         store_y(0, 0, 2)
         quantize_h(3)
         for quad in range(QUADS):
-            nc.gpsimd.dma_start(
+            nc.scalar.dma_start(
                 out=out_3[0, 4 * quad : 4 * quad + 4, :].bitcast(I32),
                 in_=h_plane[32 * quad : 32 * quad + 4, :].bitcast(I32),
             )

@@ -29,7 +29,7 @@ ALIGN = 256
 
 V4_ROW, V8_ROW, WG_ROW = 0, 4, 8
 
-STEPS = [(chunk, pair) for chunk in range(4) for pair in range(2)]
+STEPS = [(0, 0), (0, 1), (1, 0), (1, 1), (2, 0), (3, 0), (2, 1), (3, 1)]
 EARLY = 3
 
 
@@ -75,11 +75,11 @@ def tile_mix_glusave_sigm_res_mul_kernel(
         x_plane = [tile("x_plane%d" % half, [P, HALF], U8) for half in range(2)]
         g_sb = tile("g_sb", [P, N_BLOCKS, T], F32)
         gate = {step: tile("gate%d_%d" % step, [P, 2 * CHUNK], F32) for step in STEPS}
-        h = [tile("h%d" % half, [P, PACK, HALF], F32) for half in range(2)]
+        h = tile("h", [P, PACK, T], F32)
         h_bf = [tile("h_bf%d" % half, [P, PACK * HALF], BF16) for half in range(2)]
-        h_codes = [tile("h_codes%d" % half, [P, HALF], U32) for half in range(2)]
+        h_codes = tile("h_codes", [P, T], U32)
         h_plane = tile("h_plane", [P, T], U8)
-        y = [tile("y%d" % half, [P, N_BLOCKS, HALF], F32) for half in range(2)]
+        y = tile("y", [P, N_BLOCKS, T], F32)
 
         def half_cols(half):
             return slice(half * HALF, (half + 1) * HALF)
@@ -114,12 +114,10 @@ def tile_mix_glusave_sigm_res_mul_kernel(
         def quantize_h(chunk):
             half, first = place(chunk)
             quantize(
-                h_codes[half][:, first : first + CHUNK],
+                h_codes[:, chunk * CHUNK : (chunk + 1) * CHUNK],
                 h_plane[:, chunk * CHUNK : (chunk + 1) * CHUNK],
                 h_bf[half][:, PACK * first : PACK * (first + CHUNK)],
             )
-            if chunk % 2 == 1:
-                nc.sync.dma_start(out=h_word_rows[:, half_cols(half)], in_=h_codes[half][:].bitcast(I32))
 
         def first_layer(codes, plane, row, step):
             chunk, pair = step
@@ -149,27 +147,81 @@ def tile_mix_glusave_sigm_res_mul_kernel(
 
         def hidden(step, ub):
             chunk, pair = step
-            half, first = place(chunk)
             rows = slice(2 * pair, 2 * pair + 2)
             nc.vector.tensor_tensor(
-                out=h[half][:, rows, first : first + CHUNK],
+                out=h[:, rows, chunk * CHUNK : (chunk + 1) * CHUNK],
                 in0=ub[:].rearrange("p (j t) -> p j t", j=2),
                 in1=gate[step][:].rearrange("p (j t) -> p j t", j=2),
                 op=MULT,
             )
-            if chunk % 2 == 1:
-                nc.sync.dma_start(out=h_rows[:, rows, half_cols(half)], in_=h[half][:, rows, :])
+
+        def round_wu(copy, pair):
+            js = slice(2 * pair, 2 * pair + 2)
+            copy(
+                out=wu_bf[:].rearrange("p (j m i) -> p m i j", j=PACK, i=PACK)[:, :, :, js],
+                in_=wu_raw[:].rearrange("p i (m j) -> p m i j", j=PACK)[:, :, :, js],
+            )
+
+        def quantize_wu(pair):
+            cols = slice(2 * pair * P, 2 * (pair + 1) * P)
+            quantize(wu_codes[:, cols], wu_plane[:, cols], wu_bf[:, PACK * cols.start : PACK * cols.stop])
+
+        def interleave_gpsimd(dst, src, first, last):
+            nc.gpsimd.tensor_scalar(
+                out=dst[:, PACK * first : PACK * last].rearrange("p (c j) -> p c j", j=PACK),
+                in0=src[:, :, first:last].rearrange("p j c -> p c j"),
+                scalar1=1.0,
+                scalar2=-0.0,
+                op0=MULT,
+                op1=ADD,
+            )
+
+        def round_h(engine, first, last):
+            half = first // HALF
+            src = h[:, :, half_cols(half)]
+            if engine == "g":
+                interleave_gpsimd(h_bf[half], src, first - half * HALF, last - half * HALF)
+            else:
+                copy = nc.scalar.copy if engine == "s" else nc.vector.tensor_copy
+                interleave(copy, h_bf[half], src, first - half * HALF, last - half * HALF)
+
+        def quantize_h_half(half):
+            quantize(h_codes[:, half_cols(half)], h_plane[:, half_cols(half)], h_bf[half][:])
+
+        def deal(dealt_tile, raw_tile):
+            nc.vector.tensor_copy(
+                out=dealt_tile[:].rearrange("p (j m) -> p j m", j=PACK),
+                in_=raw_tile[:].rearrange("p (m j) -> p j m", j=PACK),
+            )
+
+        def store_h(j0, j1, first, last):
+            nc.sync.dma_start(out=h_rows[:, j0:j1, first:last], in_=h[:, j0:j1, first:last])
+
+        def store_words(first, last):
+            nc.sync.dma_start(out=h_word_rows[:, first:last], in_=h_codes[:, first:last].bitcast(I32))
+
+        def store_planes():
+            for quad in range(QUADS):
+                nc.scalar.dma_start(
+                    out=out_3[0, 4 * quad : 4 * quad + 4, :].bitcast(I32),
+                    in_=h_plane[32 * quad : 32 * quad + 4, :].bitcast(I32),
+                )
+
+        def both(step):
+            ga = gate_sums(step)
+            ub[step] = up_sums(step)
+            sigmoid(step, ga)
 
         def round_h_scalar(chunk):
             half, first = place(chunk)
-            interleave(nc.scalar.copy, h_bf[half], h[half], first, first + PIECE)
+            interleave(nc.scalar.copy, h_bf[half], h[:, :, half_cols(half)], first, first + PIECE)
 
         def round_h_gpsimd(chunk):
             half, first = place(chunk)
             piece = slice(first + PIECE, first + CHUNK)
             nc.gpsimd.tensor_scalar(
                 out=h_bf[half][:, PACK * piece.start : PACK * piece.stop].rearrange("p (c j) -> p c j", j=PACK),
-                in0=h[half][:, :, piece].rearrange("p j c -> p c j"),
+                in0=h[:, :, half_cols(half)][:, :, piece].rearrange("p j c -> p c j"),
                 scalar1=1.0,
                 scalar2=-0.0,
                 op0=MULT,
@@ -183,7 +235,7 @@ def tile_mix_glusave_sigm_res_mul_kernel(
                 out=acc[:],
                 lhsT=v4_codes[:, 2 * n_cols.start : 2 * n_cols.stop].bitcast(FP4X4),
                 lhsT_scale=v_planes[V4_ROW:P, n_cols],
-                rhs=h_codes[half][:].bitcast(FP8X4),
+                rhs=h_codes[:, half_cols(half)].bitcast(FP8X4),
                 rhs_scale=h_plane[:, half_cols(half)],
                 start=True,
                 stop=False,
@@ -192,15 +244,15 @@ def tile_mix_glusave_sigm_res_mul_kernel(
                 out=acc[:],
                 lhsT=v8_codes[:, n_cols].bitcast(FP8X4),
                 lhsT_scale=v_planes[V8_ROW:P, n_cols],
-                rhs=h_codes[half][:].bitcast(FP8X4),
+                rhs=h_codes[:, half_cols(half)].bitcast(FP8X4),
                 rhs_scale=h_plane[:, half_cols(half)],
                 start=False,
                 stop=True,
             )
-            nc.vector.tensor_tensor(out=y[half][:, block, :], in0=acc[:], in1=g_sb[:, block, half_cols(half)], op=MULT)
+            nc.vector.tensor_tensor(out=y[:, block, half_cols(half)], in0=acc[:], in1=g_sb[:, block, half_cols(half)], op=MULT)
 
         def store_y(half, first, last):
-            nc.sync.dma_start(out=y_rows[:, first:last, half_cols(half)], in_=y[half][:, first:last, :])
+            nc.sync.dma_start(out=y_rows[:, first:last, half_cols(half)], in_=y[:, first:last, half_cols(half)])
 
         nc.vector.memset(wg_plane_raw[:].bitcast(I32), 0)
         nc.gpsimd.memset(v_planes[:].bitcast(I32), 0)
@@ -218,62 +270,63 @@ def tile_mix_glusave_sigm_res_mul_kernel(
 
         interleave(nc.vector.tensor_copy, x_bf[0], x_raw[0], 0, CHUNK)
         interleave(nc.scalar.copy, x_bf[0], x_raw[0], CHUNK, HALF)
-        for dealt_tile, raw_tile in ((wg_plane, wg_plane_raw), (wg_codes, wg_raw)):
-            nc.vector.tensor_copy(
-                out=dealt_tile[:].rearrange("p (j m) -> p j m", j=PACK),
-                in_=raw_tile[:].rearrange("p (m j) -> p j m", j=PACK),
-            )
+        deal(wg_plane, wg_plane_raw)
         quantize_x(0)
+        deal(wg_codes, wg_raw)
         quantize_x(1)
-        for step in STEPS[:EARLY]:
+        for step in ((0, 0), (0, 1), (1, 0), (1, 1)):
             sigmoid(step, gate_sums(step))
-
-        nc.vector.tensor_copy(
-            out=wu_bf[:].rearrange("p (j m i) -> p m i j", j=PACK, i=PACK),
-            in_=wu_raw[:].rearrange("p i (m j) -> p m i j", j=PACK),
-        )
-        for pair in range(2):
-            cols = slice(2 * pair * P, 2 * (pair + 1) * P)
-            quantize(wu_codes[:, cols], wu_plane[:, cols], wu_bf[:, PACK * cols.start : PACK * cols.stop])
-        early_ub = [up_sums(step) for step in STEPS[:EARLY]]
-
+        round_wu(nc.vector.tensor_copy, 0)
+        round_wu(nc.vector.tensor_copy, 1)
+        quantize_wu(0)
+        quantize_wu(1)
+        ub = {step: up_sums(step) for step in ((0, 0), (0, 1), (1, 0), (1, 1))}
         interleave(nc.vector.tensor_copy, x_bf[1], x_raw[1], 0, PIECE)
         interleave(nc.scalar.copy, x_bf[1], x_raw[1], PIECE, CHUNK)
         interleave(nc.scalar.copy, x_bf[1], x_raw[1], CHUNK, HALF)
-        hidden(STEPS[0], early_ub[0])
-        hidden(STEPS[1], early_ub[1])
-        round_h_gpsimd(0)
+        hidden((0, 0), ub[(0, 0)])
+        hidden((0, 1), ub[(0, 1)])
+        round_h("g", 128, 256)
         quantize_x(2)
-        hidden(STEPS[2], early_ub[2])
+        hidden((1, 0), ub[(1, 0)])
+        store_h(0, 2, 0, 512)
         quantize_x(3)
-
-        for step in STEPS[EARLY:]:
-            chunk, pair = step
-            ga = gate_sums(step)
-            ub = up_sums(step)
-            sigmoid(step, ga)
-            hidden(step, ub)
-            if pair == 1:
-                round_h_scalar(chunk - 1)
-                round_h_gpsimd(chunk)
-                quantize_h(chunk - 1)
-        round_h_scalar(3)
-
+        hidden((1, 1), ub[(1, 1)])
+        store_h(2, 4, 0, 512)
+        round_h("s", 0, 128)
+        round_h("g", 384, 512)
+        quantize_h(0)
+        both((2, 0))
+        hidden((2, 0), ub[(2, 0)])
+        both((2, 1))
+        hidden((2, 1), ub[(2, 1)])
+        store_h(0, 4, 512, 768)
+        round_h("s", 256, 384)
+        round_h("g", 640, 768)
+        quantize_h(1)
+        store_words(0, 512)
+        both((3, 0))
+        hidden((3, 0), ub[(3, 0)])
+        both((3, 1))
+        hidden((3, 1), ub[(3, 1)])
+        store_h(0, 4, 768, 1024)
+        round_h("s", 512, 640)
+        round_h("g", 896, 1024)
+        round_h("s", 768, 896)
         last_layer(0, 0)
         last_layer(0, 1)
         store_y(0, 0, 2)
+        quantize_h(2)
         quantize_h(3)
-        for quad in range(QUADS):
-            nc.scalar.dma_start(
-                out=out_3[0, 4 * quad : 4 * quad + 4, :].bitcast(I32),
-                in_=h_plane[32 * quad : 32 * quad + 4, :].bitcast(I32),
-            )
+        store_words(512, 1024)
+        store_planes()
         last_layer(0, 2)
         last_layer(0, 3)
         store_y(0, 2, 4)
         last_layer(1, 0)
         last_layer(1, 1)
         store_y(1, 0, 2)
-        for block in range(2, N_BLOCKS):
-            last_layer(1, block)
-            store_y(1, block, block + 1)
+        last_layer(1, 2)
+        store_y(1, 2, 3)
+        last_layer(1, 3)
+        store_y(1, 3, 4)

@@ -197,8 +197,8 @@ def tile_mix_glusave_sigm_res_mul_kernel(
         def store_h(j0, j1, first, last):
             nc.sync.dma_start(out=h_rows[:, j0:j1, first:last], in_=h[:, j0:j1, first:last])
 
-        def store_words(first, last):
-            nc.sync.dma_start(out=h_word_rows[:, first:last], in_=h_codes[:, first:last].bitcast(I32))
+        def store_words(first, last, queue=nc.sync):
+            queue.dma_start(out=h_word_rows[:, first:last], in_=h_codes[:, first:last].bitcast(I32))
 
         def store_planes():
             for quad in range(QUADS):
@@ -251,8 +251,11 @@ def tile_mix_glusave_sigm_res_mul_kernel(
             )
             nc.vector.tensor_tensor(out=y[:, block, half_cols(half)], in0=acc[:], in1=g_sb[:, block, half_cols(half)], op=MULT)
 
-        def store_y(half, first, last):
-            nc.sync.dma_start(out=y_rows[:, first:last, half_cols(half)], in_=y[:, first:last, half_cols(half)])
+        def store_rows(first, last):
+            nc.sync.dma_start(out=y_rows[:, first:last, :], in_=y[:, first:last, :])
+
+        def store_y(half, first, last, queue=nc.sync):
+            queue.dma_start(out=y_rows[:, first:last, half_cols(half)], in_=y[:, first:last, half_cols(half)])
 
         nc.vector.memset(wg_plane_raw[:].bitcast(I32), 0)
         nc.gpsimd.memset(v_planes[:].bitcast(I32), 0)
@@ -266,7 +269,7 @@ def tile_mix_glusave_sigm_res_mul_kernel(
         load_plane(nc.gpsimd, v_planes, V8_ROW, v8_scales)
         nc.sync.dma_start(out=v4_codes[:].bitcast(I32), in_=v4_words[0].bitcast(I32))
         nc.sync.dma_start(out=v8_codes[:].bitcast(I32), in_=v8_words[0].rearrange("p n i -> p (n i)").bitcast(I32))
-        nc.sync.dma_start(out=g_sb[:], in_=g_rows)
+        nc.sync.dma_start(out=g_sb[:, 0:2, :], in_=g_rows[:, 0:2, :])
 
         interleave(nc.vector.tensor_copy, x_bf[0], x_raw[0], 0, CHUNK)
         interleave(nc.scalar.copy, x_bf[0], x_raw[0], CHUNK, HALF)
@@ -274,8 +277,10 @@ def tile_mix_glusave_sigm_res_mul_kernel(
         quantize_x(0)
         deal(wg_codes, wg_raw)
         quantize_x(1)
-        for step in ((0, 0), (0, 1), (1, 0), (1, 1)):
+        for step in ((0, 0), (0, 1), (1, 0)):
             sigmoid(step, gate_sums(step))
+        nc.scalar.dma_start(out=g_sb[:, 2:4, :], in_=g_rows[:, 2:4, :])
+        sigmoid((1, 1), gate_sums((1, 1)))
         round_wu(nc.vector.tensor_copy, 0)
         round_wu(nc.vector.tensor_copy, 1)
         quantize_wu(0)
@@ -300,16 +305,16 @@ def tile_mix_glusave_sigm_res_mul_kernel(
         hidden((2, 0), ub[(2, 0)])
         both((2, 1))
         hidden((2, 1), ub[(2, 1)])
-        store_h(0, 4, 512, 768)
         round_h("s", 256, 384)
         round_h("g", 640, 768)
         quantize_h(1)
         store_words(0, 512)
         both((3, 0))
         hidden((3, 0), ub[(3, 0)])
+        store_h(0, 2, 512, 1024)
         both((3, 1))
         hidden((3, 1), ub[(3, 1)])
-        store_h(0, 4, 768, 1024)
+        store_h(2, 4, 512, 1024)
         round_h("s", 512, 640)
         round_h("g", 896, 1024)
         round_h("s", 768, 896)
@@ -318,15 +323,14 @@ def tile_mix_glusave_sigm_res_mul_kernel(
         store_y(0, 0, 2)
         quantize_h(2)
         quantize_h(3)
-        store_words(512, 1024)
+        store_words(512, 1024, nc.scalar)
         store_planes()
         last_layer(0, 2)
         last_layer(0, 3)
         store_y(0, 2, 4)
         last_layer(1, 0)
         last_layer(1, 1)
-        store_y(1, 0, 2)
+        store_y(1, 0, 2, nc.scalar)
         last_layer(1, 2)
-        store_y(1, 2, 3)
         last_layer(1, 3)
-        store_y(1, 3, 4)
+        store_y(1, 2, 4)

@@ -197,12 +197,12 @@ def tile_mix_glusave_sigm_res_mul_kernel(
         def store_h(j0, j1, first, last):
             nc.sync.dma_start(out=h_rows[:, j0:j1, first:last], in_=h[:, j0:j1, first:last])
 
-        def store_words(first, last, queue=nc.sync):
-            queue.dma_start(out=h_word_rows[:, first:last], in_=h_codes[:, first:last].bitcast(I32))
+        def store_words(first, last):
+            nc.sync.dma_start(out=h_word_rows[:, first:last], in_=h_codes[:, first:last].bitcast(I32))
 
         def store_planes():
             for quad in range(QUADS):
-                nc.scalar.dma_start(
+                nc.sync.dma_start(
                     out=out_3[0, 4 * quad : 4 * quad + 4, :].bitcast(I32),
                     in_=h_plane[32 * quad : 32 * quad + 4, :].bitcast(I32),
                 )
@@ -254,8 +254,8 @@ def tile_mix_glusave_sigm_res_mul_kernel(
         def store_rows(first, last):
             nc.sync.dma_start(out=y_rows[:, first:last, :], in_=y[:, first:last, :])
 
-        def store_y(half, first, last, queue=nc.sync):
-            queue.dma_start(out=y_rows[:, first:last, half_cols(half)], in_=y[:, first:last, half_cols(half)])
+        def store_y(half, first, last):
+            nc.sync.dma_start(out=y_rows[:, first:last, half_cols(half)], in_=y[:, first:last, half_cols(half)])
 
         nc.vector.memset(wg_plane_raw[:].bitcast(I32), 0)
         nc.gpsimd.memset(v_planes[:].bitcast(I32), 0)
@@ -269,7 +269,7 @@ def tile_mix_glusave_sigm_res_mul_kernel(
         load_plane(nc.gpsimd, v_planes, V8_ROW, v8_scales)
         nc.sync.dma_start(out=v4_codes[:].bitcast(I32), in_=v4_words[0].bitcast(I32))
         nc.sync.dma_start(out=v8_codes[:].bitcast(I32), in_=v8_words[0].rearrange("p n i -> p (n i)").bitcast(I32))
-        nc.sync.dma_start(out=g_sb[:, 0:2, :], in_=g_rows[:, 0:2, :])
+        nc.sync.dma_start(out=g_sb[:], in_=g_rows)
 
         interleave(nc.vector.tensor_copy, x_bf[0], x_raw[0], 0, CHUNK)
         interleave(nc.scalar.copy, x_bf[0], x_raw[0], CHUNK, HALF)
@@ -277,10 +277,8 @@ def tile_mix_glusave_sigm_res_mul_kernel(
         quantize_x(0)
         deal(wg_codes, wg_raw)
         quantize_x(1)
-        for step in ((0, 0), (0, 1), (1, 0)):
+        for step in ((0, 0), (0, 1), (1, 0), (1, 1)):
             sigmoid(step, gate_sums(step))
-        nc.scalar.dma_start(out=g_sb[:, 2:4, :], in_=g_rows[:, 2:4, :])
-        sigmoid((1, 1), gate_sums((1, 1)))
         round_wu(nc.vector.tensor_copy, 0)
         round_wu(nc.vector.tensor_copy, 1)
         quantize_wu(0)
@@ -323,14 +321,14 @@ def tile_mix_glusave_sigm_res_mul_kernel(
         store_y(0, 0, 2)
         quantize_h(2)
         quantize_h(3)
-        store_words(512, 1024, nc.scalar)
-        store_planes()
+        store_words(512, 1024)
         last_layer(0, 2)
         last_layer(0, 3)
         store_y(0, 2, 4)
         last_layer(1, 0)
         last_layer(1, 1)
-        store_y(1, 0, 2, nc.scalar)
+        store_y(1, 0, 2)
         last_layer(1, 2)
         last_layer(1, 3)
         store_y(1, 2, 4)
+        store_planes()

@@ -265,11 +265,11 @@ def tile_mix_glusave_sigm_res_mul_kernel(
         nc.sync.dma_start(out=wg_raw[:], in_=wg_words[0].rearrange("p r i -> p (r i)").bitcast(I32))
         nc.sync.dma_start(out=wu_raw[:], in_=wu.rearrange("(p j) r -> p j r", j=PACK))
         nc.sync.dma_start(out=x_raw[1][:], in_=x_rows[:, :, half_cols(1)])
-        load_plane(nc.gpsimd, v_planes, V4_ROW, v4_scales)
-        load_plane(nc.gpsimd, v_planes, V8_ROW, v8_scales)
+        load_plane(nc.sync, v_planes, V4_ROW, v4_scales)
+        nc.sync.dma_start(out=g_sb[:], in_=g_rows)
         nc.sync.dma_start(out=v4_codes[:].bitcast(I32), in_=v4_words[0].bitcast(I32))
         nc.sync.dma_start(out=v8_codes[:].bitcast(I32), in_=v8_words[0].rearrange("p n i -> p (n i)").bitcast(I32))
-        nc.sync.dma_start(out=g_sb[:], in_=g_rows)
+        load_plane(nc.sync, v_planes, V8_ROW, v8_scales)
 
         interleave(nc.vector.tensor_copy, x_bf[0], x_raw[0], 0, CHUNK)
         interleave(nc.scalar.copy, x_bf[0], x_raw[0], CHUNK, HALF)

@@ -29,8 +29,7 @@ ALIGN = 256
 
 V4_ROW, V8_ROW, WG_ROW = 0, 4, 8
 
-STEPS = [(0, 0), (0, 1), (1, 0), (1, 1), (2, 0), (3, 0), (2, 1), (3, 1)]
-EARLY = 3
+FIRST_STEPS = [(chunk, pair) for chunk in (0, 1) for pair in range(2)]
 
 
 def tile_mix_glusave_sigm_res_mul_kernel(
@@ -74,7 +73,7 @@ def tile_mix_glusave_sigm_res_mul_kernel(
         x_codes = [tile("x_codes%d" % half, [P, HALF], U32) for half in range(2)]
         x_plane = [tile("x_plane%d" % half, [P, HALF], U8) for half in range(2)]
         g_sb = tile("g_sb", [P, N_BLOCKS, T], F32)
-        gate = {step: tile("gate%d_%d" % step, [P, 2 * CHUNK], F32) for step in STEPS}
+        gate = {step: tile("gate%d_%d" % step, [P, 2 * CHUNK], F32) for step in [(chunk, pair) for chunk in range(4) for pair in range(2)]}
         h = tile("h", [P, PACK, T], F32)
         h_bf = [tile("h_bf%d" % half, [P, PACK * HALF], BF16) for half in range(2)]
         h_codes = tile("h_codes", [P, T], U32)
@@ -84,12 +83,18 @@ def tile_mix_glusave_sigm_res_mul_kernel(
         def half_cols(half):
             return slice(half * HALF, (half + 1) * HALF)
 
+        def chunk_cols(chunk):
+            return slice(chunk * CHUNK, (chunk + 1) * CHUNK)
+
+        def pair_rows(pair):
+            return slice(2 * pair, 2 * pair + 2)
+
         def place(chunk):
             return chunk // 2, (chunk % 2) * CHUNK
 
-        def load_plane(engine, plane, row, scales):
+        def load_plane(plane, row, scales):
             for quad in range(QUADS):
-                engine.dma_start(
+                nc.sync.dma_start(
                     out=plane[32 * quad + row : 32 * quad + row + 4, :].bitcast(I32),
                     in_=scales[0, 4 * quad : 4 * quad + 4, :].bitcast(I32),
                 )
@@ -98,6 +103,12 @@ def tile_mix_glusave_sigm_res_mul_kernel(
             copy(
                 out=dst[:, PACK * first : PACK * last].rearrange("p (c i j) -> p c j i", i=LINE, j=PACK),
                 in_=src[:, :, first:last].rearrange("p j (c i) -> p c j i", i=LINE),
+            )
+
+        def deal(dealt, raw):
+            nc.vector.tensor_copy(
+                out=dealt[:].rearrange("p (j m) -> p j m", j=PACK),
+                in_=raw[:].rearrange("p (m j) -> p j m", j=PACK),
             )
 
         def quantize(codes, plane, src):
@@ -111,13 +122,20 @@ def tile_mix_glusave_sigm_res_mul_kernel(
                 x_bf[half][:, PACK * first : PACK * (first + CHUNK)],
             )
 
-        def quantize_h(chunk):
-            half, first = place(chunk)
-            quantize(
-                h_codes[:, chunk * CHUNK : (chunk + 1) * CHUNK],
-                h_plane[:, chunk * CHUNK : (chunk + 1) * CHUNK],
-                h_bf[half][:, PACK * first : PACK * (first + CHUNK)],
+        def round_wu(pair):
+            nc.vector.tensor_copy(
+                out=wu_bf[:].rearrange("p (j m i) -> p m i j", j=PACK, i=PACK)[:, :, :, pair_rows(pair)],
+                in_=wu_raw[:].rearrange("p i (m j) -> p m i j", j=PACK)[:, :, :, pair_rows(pair)],
             )
+
+        def quantize_wu(pair):
+            cols = slice(2 * pair * P, 2 * (pair + 1) * P)
+            quantize(wu_codes[:, cols], wu_plane[:, cols], wu_bf[:, PACK * cols.start : PACK * cols.stop])
+
+        def quantize_h(chunk, chunks):
+            half, first = place(chunk)
+            cols = slice(chunk * CHUNK, (chunk + chunks) * CHUNK)
+            quantize(h_codes[:, cols], h_plane[:, cols], h_bf[half][:, PACK * first : PACK * (first + chunks * CHUNK)])
 
         def first_layer(codes, plane, row, step):
             chunk, pair = step
@@ -147,70 +165,18 @@ def tile_mix_glusave_sigm_res_mul_kernel(
 
         def hidden(step, ub):
             chunk, pair = step
-            rows = slice(2 * pair, 2 * pair + 2)
             nc.vector.tensor_tensor(
-                out=h[:, rows, chunk * CHUNK : (chunk + 1) * CHUNK],
+                out=h[:, pair_rows(pair), chunk_cols(chunk)],
                 in0=ub[:].rearrange("p (j t) -> p j t", j=2),
                 in1=gate[step][:].rearrange("p (j t) -> p j t", j=2),
                 op=MULT,
             )
 
-        def round_wu(copy, pair):
-            js = slice(2 * pair, 2 * pair + 2)
-            copy(
-                out=wu_bf[:].rearrange("p (j m i) -> p m i j", j=PACK, i=PACK)[:, :, :, js],
-                in_=wu_raw[:].rearrange("p i (m j) -> p m i j", j=PACK)[:, :, :, js],
-            )
-
-        def quantize_wu(pair):
-            cols = slice(2 * pair * P, 2 * (pair + 1) * P)
-            quantize(wu_codes[:, cols], wu_plane[:, cols], wu_bf[:, PACK * cols.start : PACK * cols.stop])
-
-        def interleave_gpsimd(dst, src, first, last):
-            nc.gpsimd.tensor_scalar(
-                out=dst[:, PACK * first : PACK * last].rearrange("p (c j) -> p c j", j=PACK),
-                in0=src[:, :, first:last].rearrange("p j c -> p c j"),
-                scalar1=1.0,
-                scalar2=-0.0,
-                op0=MULT,
-                op1=ADD,
-            )
-
-        def round_h(engine, first, last):
-            half = first // HALF
-            src = h[:, :, half_cols(half)]
-            if engine == "g":
-                interleave_gpsimd(h_bf[half], src, first - half * HALF, last - half * HALF)
-            else:
-                copy = nc.scalar.copy if engine == "s" else nc.vector.tensor_copy
-                interleave(copy, h_bf[half], src, first - half * HALF, last - half * HALF)
-
-        def quantize_h_half(half):
-            quantize(h_codes[:, half_cols(half)], h_plane[:, half_cols(half)], h_bf[half][:])
-
-        def deal(dealt_tile, raw_tile):
-            nc.vector.tensor_copy(
-                out=dealt_tile[:].rearrange("p (j m) -> p j m", j=PACK),
-                in_=raw_tile[:].rearrange("p (m j) -> p j m", j=PACK),
-            )
-
-        def store_h(j0, j1, first, last):
-            nc.sync.dma_start(out=h_rows[:, j0:j1, first:last], in_=h[:, j0:j1, first:last])
-
-        def store_words(first, last):
-            nc.sync.dma_start(out=h_word_rows[:, first:last], in_=h_codes[:, first:last].bitcast(I32))
-
-        def store_planes():
-            for quad in range(QUADS):
-                nc.sync.dma_start(
-                    out=out_3[0, 4 * quad : 4 * quad + 4, :].bitcast(I32),
-                    in_=h_plane[32 * quad : 32 * quad + 4, :].bitcast(I32),
-                )
-
-        def both(step):
+        def whole_step(step):
             ga = gate_sums(step)
-            ub[step] = up_sums(step)
+            ub = up_sums(step)
             sigmoid(step, ga)
+            hidden(step, ub)
 
         def round_h_scalar(chunk):
             half, first = place(chunk)
@@ -249,27 +215,35 @@ def tile_mix_glusave_sigm_res_mul_kernel(
                 start=False,
                 stop=True,
             )
-            nc.vector.tensor_tensor(out=y[:, block, half_cols(half)], in0=acc[:], in1=g_sb[:, block, half_cols(half)], op=MULT)
+            nc.vector.tensor_tensor(
+                out=y[:, block, half_cols(half)], in0=acc[:], in1=g_sb[:, block, half_cols(half)], op=MULT
+            )
 
-        def store_rows(first, last):
-            nc.sync.dma_start(out=y_rows[:, first:last, :], in_=y[:, first:last, :])
+        def last_pair(half, pair):
+            blocks = pair_rows(pair)
+            for block in range(blocks.start, blocks.stop):
+                last_layer(half, block)
+            nc.sync.dma_start(out=y_rows[:, blocks, half_cols(half)], in_=y[:, blocks, half_cols(half)])
 
-        def store_y(half, first, last):
-            nc.sync.dma_start(out=y_rows[:, first:last, half_cols(half)], in_=y[:, first:last, half_cols(half)])
+        def store_h(rows, half):
+            nc.sync.dma_start(out=h_rows[:, rows, half_cols(half)], in_=h[:, rows, half_cols(half)])
+
+        def store_words(half):
+            nc.sync.dma_start(out=h_word_rows[:, half_cols(half)], in_=h_codes[:, half_cols(half)].bitcast(I32))
 
         nc.vector.memset(wg_plane_raw[:].bitcast(I32), 0)
         nc.gpsimd.memset(v_planes[:].bitcast(I32), 0)
 
         nc.sync.dma_start(out=x_raw[0][:], in_=x_rows[:, :, half_cols(0)])
-        load_plane(nc.sync, wg_plane_raw, WG_ROW, wg_scales)
+        load_plane(wg_plane_raw, WG_ROW, wg_scales)
         nc.sync.dma_start(out=wg_raw[:], in_=wg_words[0].rearrange("p r i -> p (r i)").bitcast(I32))
         nc.sync.dma_start(out=wu_raw[:], in_=wu.rearrange("(p j) r -> p j r", j=PACK))
         nc.sync.dma_start(out=x_raw[1][:], in_=x_rows[:, :, half_cols(1)])
-        load_plane(nc.sync, v_planes, V4_ROW, v4_scales)
+        load_plane(v_planes, V4_ROW, v4_scales)
         nc.sync.dma_start(out=g_sb[:], in_=g_rows)
         nc.sync.dma_start(out=v4_codes[:].bitcast(I32), in_=v4_words[0].bitcast(I32))
         nc.sync.dma_start(out=v8_codes[:].bitcast(I32), in_=v8_words[0].rearrange("p n i -> p (n i)").bitcast(I32))
-        load_plane(nc.sync, v_planes, V8_ROW, v8_scales)
+        load_plane(v_planes, V8_ROW, v8_scales)
 
         interleave(nc.vector.tensor_copy, x_bf[0], x_raw[0], 0, CHUNK)
         interleave(nc.scalar.copy, x_bf[0], x_raw[0], CHUNK, HALF)
@@ -277,58 +251,50 @@ def tile_mix_glusave_sigm_res_mul_kernel(
         quantize_x(0)
         deal(wg_codes, wg_raw)
         quantize_x(1)
-        for step in ((0, 0), (0, 1), (1, 0), (1, 1)):
+        for step in FIRST_STEPS:
             sigmoid(step, gate_sums(step))
-        round_wu(nc.vector.tensor_copy, 0)
-        round_wu(nc.vector.tensor_copy, 1)
-        quantize_wu(0)
-        quantize_wu(1)
-        ub = {step: up_sums(step) for step in ((0, 0), (0, 1), (1, 0), (1, 1))}
+
+        for pair in range(2):
+            round_wu(pair)
+        for pair in range(2):
+            quantize_wu(pair)
+        first_ub = {step: up_sums(step) for step in FIRST_STEPS}
+
         interleave(nc.vector.tensor_copy, x_bf[1], x_raw[1], 0, PIECE)
         interleave(nc.scalar.copy, x_bf[1], x_raw[1], PIECE, CHUNK)
         interleave(nc.scalar.copy, x_bf[1], x_raw[1], CHUNK, HALF)
-        hidden((0, 0), ub[(0, 0)])
-        hidden((0, 1), ub[(0, 1)])
-        round_h("g", 128, 256)
-        quantize_x(2)
-        hidden((1, 0), ub[(1, 0)])
-        store_h(0, 2, 0, 512)
-        quantize_x(3)
-        hidden((1, 1), ub[(1, 1)])
-        store_h(2, 4, 0, 512)
-        round_h("s", 0, 128)
-        round_h("g", 384, 512)
-        quantize_h(0)
-        both((2, 0))
-        hidden((2, 0), ub[(2, 0)])
-        both((2, 1))
-        hidden((2, 1), ub[(2, 1)])
-        round_h("s", 256, 384)
-        round_h("g", 640, 768)
-        quantize_h(1)
-        store_words(0, 512)
-        both((3, 0))
-        hidden((3, 0), ub[(3, 0)])
-        store_h(0, 2, 512, 1024)
-        both((3, 1))
-        hidden((3, 1), ub[(3, 1)])
-        store_h(2, 4, 512, 1024)
-        round_h("s", 512, 640)
-        round_h("g", 896, 1024)
-        round_h("s", 768, 896)
-        last_layer(0, 0)
-        last_layer(0, 1)
-        store_y(0, 0, 2)
-        quantize_h(2)
-        quantize_h(3)
-        store_words(512, 1024)
-        last_layer(0, 2)
-        last_layer(0, 3)
-        store_y(0, 2, 4)
-        last_layer(1, 0)
-        last_layer(1, 1)
-        store_y(1, 0, 2)
-        last_layer(1, 2)
-        last_layer(1, 3)
-        store_y(1, 2, 4)
-        store_planes()
+
+        for chunk in range(2):
+            for pair in range(2):
+                hidden((chunk, pair), first_ub[(chunk, pair)])
+            if chunk == 1:
+                store_h(slice(0, PACK), 0)
+            quantize_x(chunk + 2)
+            round_h_gpsimd(chunk)
+        round_h_scalar(0)
+        for pair in range(2):
+            whole_step((2, pair))
+        round_h_scalar(1)
+        round_h_gpsimd(2)
+        quantize_h(0, 2)
+        store_words(0)
+        for pair in range(2):
+            whole_step((3, pair))
+            store_h(pair_rows(pair), 1)
+        round_h_scalar(2)
+        round_h_gpsimd(3)
+        round_h_scalar(3)
+
+        last_pair(0, 0)
+        quantize_h(2, 1)
+        quantize_h(3, 1)
+        store_words(1)
+        last_pair(0, 1)
+        last_pair(1, 0)
+        last_pair(1, 1)
+
+        for quad in range(QUADS):
+            nc.sync.dma_start(
+                out=out_3[0, 4 * quad : 4 * quad + 4, :].bitcast(I32),
+                in_=h_plane[32 * quad : 32 * quad + 4, :].bitcast(I32),
+            )

@@ -29,7 +29,8 @@ ALIGN = 256
 
 V4_ROW, V8_ROW, WG_ROW = 0, 4, 8
 
-FIRST_STEPS = [(chunk, pair) for chunk in (0, 1) for pair in range(2)]
+ALL_STEPS = [(chunk, pair) for chunk in range(T // CHUNK) for pair in range(2)]
+FIRST_STEPS = ALL_STEPS[: len(ALL_STEPS) // 2]
 
 
 def tile_mix_glusave_sigm_res_mul_kernel(
@@ -58,7 +59,7 @@ def tile_mix_glusave_sigm_res_mul_kernel(
         h_word_rows = out_2[0].rearrange("p t i -> p (t i)").bitcast(I32)
 
         wg_raw = tile("wg_raw", [P, R], I32)
-        wg_plane_raw = tile("wg_plane_raw", [P, R], U8)
+        shared_planes = tile("shared_planes", [P, R], U8)
         wg_codes = tile("wg_codes", [P, R], I32)
         wg_plane = tile("wg_plane", [P, R], U8)
         wu_raw = tile("wu_raw", [P, PACK, R], F32)
@@ -67,13 +68,13 @@ def tile_mix_glusave_sigm_res_mul_kernel(
         wu_plane = tile("wu_plane", [P, R], U8)
         v4_codes = tile("v4_codes", [P, 2 * N], U8)
         v8_codes = tile("v8_codes", [P, N], U32)
-        v_planes = tile("v_planes", [P, N], U8)
+        v4_plane = tile("v4_plane", [P, N], U8)
         x_raw = [tile("x_raw%d" % half, [P, PACK, HALF], F32) for half in range(2)]
         x_bf = [tile("x_bf%d" % half, [P, PACK * HALF], BF16) for half in range(2)]
         x_codes = [tile("x_codes%d" % half, [P, HALF], U32) for half in range(2)]
         x_plane = [tile("x_plane%d" % half, [P, HALF], U8) for half in range(2)]
         g_sb = tile("g_sb", [P, N_BLOCKS, T], F32)
-        gate = {step: tile("gate%d_%d" % step, [P, 2 * CHUNK], F32) for step in [(chunk, pair) for chunk in range(4) for pair in range(2)]}
+        gate = {step: tile("gate%d_%d" % step, [P, 2 * CHUNK], F32) for step in ALL_STEPS}
         h = tile("h", [P, PACK, T], F32)
         h_bf = [tile("h_bf%d" % half, [P, PACK * HALF], BF16) for half in range(2)]
         h_codes = tile("h_codes", [P, T], U32)
@@ -200,7 +201,7 @@ def tile_mix_glusave_sigm_res_mul_kernel(
             nc.tensor.matmul_mx(
                 out=acc[:],
                 lhsT=v4_codes[:, 2 * n_cols.start : 2 * n_cols.stop].bitcast(FP4X4),
-                lhsT_scale=v_planes[V4_ROW:P, n_cols],
+                lhsT_scale=v4_plane[V4_ROW:P, n_cols],
                 rhs=h_codes[:, half_cols(half)].bitcast(FP8X4),
                 rhs_scale=h_plane[:, half_cols(half)],
                 start=True,
@@ -209,7 +210,7 @@ def tile_mix_glusave_sigm_res_mul_kernel(
             nc.tensor.matmul_mx(
                 out=acc[:],
                 lhsT=v8_codes[:, n_cols].bitcast(FP8X4),
-                lhsT_scale=v_planes[V8_ROW:P, n_cols],
+                lhsT_scale=shared_planes[V8_ROW:P, n_cols],
                 rhs=h_codes[:, half_cols(half)].bitcast(FP8X4),
                 rhs_scale=h_plane[:, half_cols(half)],
                 start=False,
@@ -219,11 +220,8 @@ def tile_mix_glusave_sigm_res_mul_kernel(
                 out=y[:, block, half_cols(half)], in0=acc[:], in1=g_sb[:, block, half_cols(half)], op=MULT
             )
 
-        def last_pair(half, pair):
-            blocks = pair_rows(pair)
-            for block in range(blocks.start, blocks.stop):
-                last_layer(half, block)
-            nc.sync.dma_start(out=y_rows[:, blocks, half_cols(half)], in_=y[:, blocks, half_cols(half)])
+        def store_y(blocks, cols):
+            nc.sync.dma_start(out=y_rows[:, blocks, cols], in_=y[:, blocks, cols])
 
         def store_h(rows, half):
             nc.sync.dma_start(out=h_rows[:, rows, half_cols(half)], in_=h[:, rows, half_cols(half)])
@@ -231,24 +229,24 @@ def tile_mix_glusave_sigm_res_mul_kernel(
         def store_words(half):
             nc.sync.dma_start(out=h_word_rows[:, half_cols(half)], in_=h_codes[:, half_cols(half)].bitcast(I32))
 
-        nc.vector.memset(wg_plane_raw[:].bitcast(I32), 0)
-        nc.gpsimd.memset(v_planes[:].bitcast(I32), 0)
+        nc.vector.memset(shared_planes[:].bitcast(I32), 0)
+        nc.gpsimd.memset(v4_plane[:].bitcast(I32), 0)
 
         nc.sync.dma_start(out=x_raw[0][:], in_=x_rows[:, :, half_cols(0)])
-        load_plane(wg_plane_raw, WG_ROW, wg_scales)
+        load_plane(shared_planes, WG_ROW, wg_scales)
         nc.sync.dma_start(out=wg_raw[:], in_=wg_words[0].rearrange("p r i -> p (r i)").bitcast(I32))
         nc.sync.dma_start(out=wu_raw[:], in_=wu.rearrange("(p j) r -> p j r", j=PACK))
         nc.sync.dma_start(out=x_raw[1][:], in_=x_rows[:, :, half_cols(1)])
-        load_plane(v_planes, V4_ROW, v4_scales)
+        load_plane(v4_plane, V4_ROW, v4_scales)
         nc.sync.dma_start(out=g_sb[:], in_=g_rows)
         nc.sync.dma_start(out=v4_codes[:].bitcast(I32), in_=v4_words[0].bitcast(I32))
         nc.sync.dma_start(out=v8_codes[:].bitcast(I32), in_=v8_words[0].rearrange("p n i -> p (n i)").bitcast(I32))
-        load_plane(v_planes, V8_ROW, v8_scales)
 
         interleave(nc.vector.tensor_copy, x_bf[0], x_raw[0], 0, CHUNK)
         interleave(nc.scalar.copy, x_bf[0], x_raw[0], CHUNK, HALF)
-        deal(wg_plane, wg_plane_raw)
+        deal(wg_plane, shared_planes)
         quantize_x(0)
+        load_plane(shared_planes, V8_ROW, v8_scales)
         deal(wg_codes, wg_raw)
         quantize_x(1)
         for step in FIRST_STEPS:
@@ -285,13 +283,21 @@ def tile_mix_glusave_sigm_res_mul_kernel(
         round_h_gpsimd(3)
         round_h_scalar(3)
 
-        last_pair(0, 0)
+        for block in (0, 1):
+            last_layer(0, block)
+        store_y(slice(0, 2), half_cols(0))
         quantize_h(2, 1)
         quantize_h(3, 1)
         store_words(1)
-        last_pair(0, 1)
-        last_pair(1, 0)
-        last_pair(1, 1)
+
+        for block in (2, 3):
+            last_layer(0, block)
+        for block in (2, 3):
+            last_layer(1, block)
+            store_y(slice(block, block + 1), slice(0, T))
+        for block in (0, 1):
+            last_layer(1, block)
+        store_y(slice(0, 2), half_cols(1))
 
         for quad in range(QUADS):
             nc.sync.dma_start(

from contextlib import ExitStack

import concourse.mybir as mybir

K, R, N, T = 512, 512, 512, 1024
FLOPS = 2 * T * (2 * K * R + 2 * R * N)

F32 = mybir.dt.float32
BF16 = mybir.dt.bfloat16
I32 = mybir.dt.int32
U32 = mybir.dt.uint32
U8 = mybir.dt.uint8
FP8X4 = mybir.dt.float8_e4m3fn_x4
FP4X4 = mybir.dt.float4_e2m1fn_x4
SIGMOID = mybir.ActivationFunctionType.Sigmoid
MULT = mybir.AluOpType.mult
ADD = mybir.AluOpType.add

P = 128
PACK = 4
QUADS = 4
BANKS = 8
HALF = T // 2
CHUNK = T // 4
PIECE = CHUNK // 2
LINE = 4
N_BLOCKS = N // P
ALIGN = 256

V4_ROW, V8_ROW, WG_ROW = 0, 4, 8

ALL_STEPS = [(chunk, pair) for chunk in range(T // CHUNK) for pair in range(2)]
FIRST_STEPS = ALL_STEPS[: len(ALL_STEPS) // 2]


def tile_mix_glusave_sigm_res_mul_kernel(
    tc, x, wg_words, wg_scales, wu, v4_words, v4_scales, v8_words, v8_scales, g, out_0, out_1, out_2, out_3
):
    nc = tc.nc
    with ExitStack() as ctx:
        sb = ctx.enter_context(tc.tile_pool(name="sb", bufs=1))
        ps = ctx.enter_context(tc.psum_pool(name="ps", bufs=1))
        ctx.enter_context(tc.manual_schedule())

        def tile(name, shape, dtype):
            return sb.tile(shape, dtype, name=name, align_bytes=ALIGN)

        banks_taken = []

        def next_bank():
            count = len(banks_taken)
            banks_taken.append(count)
            return ps.tile([P, HALF], F32, name="acc%d" % count, tag="bank%d" % (count % BANKS))

        x_rows = x.rearrange("(p j) t -> p j t", j=PACK)
        h_rows = out_1.rearrange("(p j) t -> p j t", j=PACK)
        g_rows = g.rearrange("(c p) t -> p c t", p=P)
        y_rows = out_0.rearrange("(c p) t -> p c t", p=P)
        h_word_rows = out_2[0].rearrange("p t i -> p (t i)").bitcast(I32)

        wg_raw = tile("wg_raw", [P, R], I32)
        shared_planes = tile("shared_planes", [P, R], U8)
        wg_codes = tile("wg_codes", [P, R], I32)
        wg_plane = tile("wg_plane", [P, R], U8)
        wu_raw = tile("wu_raw", [P, PACK, R], F32)
        wu_bf = tile("wu_bf", [P, PACK * R], BF16)
        wu_codes = tile("wu_codes", [P, R], U32)
        wu_plane = tile("wu_plane", [P, R], U8)
        v4_codes = tile("v4_codes", [P, 2 * N], U8)
        v8_codes = tile("v8_codes", [P, N], U32)
        v4_plane = tile("v4_plane", [P, N], U8)
        x_raw = [tile("x_raw%d" % half, [P, PACK, HALF], F32) for half in range(2)]
        x_bf = [tile("x_bf%d" % half, [P, PACK * HALF], BF16) for half in range(2)]
        x_codes = [tile("x_codes%d" % half, [P, HALF], U32) for half in range(2)]
        x_plane = [tile("x_plane%d" % half, [P, HALF], U8) for half in range(2)]
        g_sb = tile("g_sb", [P, N_BLOCKS, T], F32)
        gate = {step: tile("gate%d_%d" % step, [P, 2 * CHUNK], F32) for step in ALL_STEPS}
        h = tile("h", [P, PACK, T], F32)
        h_bf = [tile("h_bf%d" % half, [P, PACK * HALF], BF16) for half in range(2)]
        h_codes = tile("h_codes", [P, T], U32)
        h_plane = tile("h_plane", [P, T], U8)
        y = tile("y", [P, N_BLOCKS, T], F32)

        def half_cols(half):
            return slice(half * HALF, (half + 1) * HALF)

        def chunk_cols(chunk):
            return slice(chunk * CHUNK, (chunk + 1) * CHUNK)

        def pair_rows(pair):
            return slice(2 * pair, 2 * pair + 2)

        def place(chunk):
            return chunk // 2, (chunk % 2) * CHUNK

        def load_plane(plane, row, scales):
            for quad in range(QUADS):
                nc.sync.dma_start(
                    out=plane[32 * quad + row : 32 * quad + row + 4, :].bitcast(I32),
                    in_=scales[0, 4 * quad : 4 * quad + 4, :].bitcast(I32),
                )

        def interleave(copy, dst, src, first, last):
            copy(
                out=dst[:, PACK * first : PACK * last].rearrange("p (c i j) -> p c j i", i=LINE, j=PACK),
                in_=src[:, :, first:last].rearrange("p j (c i) -> p c j i", i=LINE),
            )

        def deal(dealt, raw):
            nc.vector.tensor_copy(
                out=dealt[:].rearrange("p (j m) -> p j m", j=PACK),
                in_=raw[:].rearrange("p (m j) -> p j m", j=PACK),
            )

        def quantize(codes, plane, src):
            nc.vector.quantize_mx(out=codes.bitcast(FP8X4), scales=plane, in_=src)

        def quantize_x(chunk):
            half, first = place(chunk)
            quantize(
                x_codes[half][:, first : first + CHUNK],
                x_plane[half][:, first : first + CHUNK],
                x_bf[half][:, PACK * first : PACK * (first + CHUNK)],
            )

        def round_wu(pair):
            nc.vector.tensor_copy(
                out=wu_bf[:].rearrange("p (j m i) -> p m i j", j=PACK, i=PACK)[:, :, :, pair_rows(pair)],
                in_=wu_raw[:].rearrange("p i (m j) -> p m i j", j=PACK)[:, :, :, pair_rows(pair)],
            )

        def quantize_wu(pair):
            cols = slice(2 * pair * P, 2 * (pair + 1) * P)
            quantize(wu_codes[:, cols], wu_plane[:, cols], wu_bf[:, PACK * cols.start : PACK * cols.stop])

        def quantize_h(chunk, chunks):
            half, first = place(chunk)
            cols = slice(chunk * CHUNK, (chunk + chunks) * CHUNK)
            quantize(h_codes[:, cols], h_plane[:, cols], h_bf[half][:, PACK * first : PACK * (first + chunks * CHUNK)])

        def first_layer(codes, plane, row, step):
            chunk, pair = step
            half, first = place(chunk)
            acc = next_bank()
            for i in range(2):
                dealt = slice((2 * pair + i) * P, (2 * pair + i + 1) * P)
                nc.tensor.matmul_mx(
                    out=acc[:, i * CHUNK : (i + 1) * CHUNK],
                    lhsT=codes[:, dealt].bitcast(FP8X4),
                    lhsT_scale=plane[row:P, dealt],
                    rhs=x_codes[half][:, first : first + CHUNK].bitcast(FP8X4),
                    rhs_scale=x_plane[half][:, first : first + CHUNK],
                    start=True,
                    stop=True,
                )
            return acc

        def gate_sums(step):
            return first_layer(wg_codes, wg_plane, WG_ROW, step)

        def up_sums(step):
            return first_layer(wu_codes, wu_plane, 0, step)

        def sigmoid(step, ga):
            nc.scalar.activation(out=gate[step][:], in_=ga[:], func=SIGMOID)

        def hidden(step, ub):
            chunk, pair = step
            nc.vector.tensor_tensor(
                out=h[:, pair_rows(pair), chunk_cols(chunk)],
                in0=ub[:].rearrange("p (j t) -> p j t", j=2),
                in1=gate[step][:].rearrange("p (j t) -> p j t", j=2),
                op=MULT,
            )

        def whole_step(step):
            ga = gate_sums(step)
            ub = up_sums(step)
            sigmoid(step, ga)
            hidden(step, ub)

        def round_h_scalar(chunk):
            half, first = place(chunk)
            interleave(nc.scalar.copy, h_bf[half], h[:, :, half_cols(half)], first, first + PIECE)

        def round_h_gpsimd(chunk):
            half, first = place(chunk)
            piece = slice(first + PIECE, first + CHUNK)
            nc.gpsimd.tensor_scalar(
                out=h_bf[half][:, PACK * piece.start : PACK * piece.stop].rearrange("p (c j) -> p c j", j=PACK),
                in0=h[:, :, half_cols(half)][:, :, piece].rearrange("p j c -> p c j"),
                scalar1=1.0,
                scalar2=-0.0,
                op0=MULT,
                op1=ADD,
            )

        def last_layer(half, block):
            acc = next_bank()
            n_cols = slice(block * P, (block + 1) * P)
            nc.tensor.matmul_mx(
                out=acc[:],
                lhsT=v4_codes[:, 2 * n_cols.start : 2 * n_cols.stop].bitcast(FP4X4),
                lhsT_scale=v4_plane[V4_ROW:P, n_cols],
                rhs=h_codes[:, half_cols(half)].bitcast(FP8X4),
                rhs_scale=h_plane[:, half_cols(half)],
                start=True,
                stop=False,
            )
            nc.tensor.matmul_mx(
                out=acc[:],
                lhsT=v8_codes[:, n_cols].bitcast(FP8X4),
                lhsT_scale=shared_planes[V8_ROW:P, n_cols],
                rhs=h_codes[:, half_cols(half)].bitcast(FP8X4),
                rhs_scale=h_plane[:, half_cols(half)],
                start=False,
                stop=True,
            )
            nc.vector.tensor_tensor(
                out=y[:, block, half_cols(half)], in0=acc[:], in1=g_sb[:, block, half_cols(half)], op=MULT
            )

        def store_y(blocks, cols):
            nc.sync.dma_start(out=y_rows[:, blocks, cols], in_=y[:, blocks, cols])

        def store_h(rows, half):
            nc.sync.dma_start(out=h_rows[:, rows, half_cols(half)], in_=h[:, rows, half_cols(half)])

        def store_words(half):
            nc.sync.dma_start(out=h_word_rows[:, half_cols(half)], in_=h_codes[:, half_cols(half)].bitcast(I32))

        nc.vector.memset(shared_planes[:].bitcast(I32), 0)
        nc.gpsimd.memset(v4_plane[:].bitcast(I32), 0)

        nc.sync.dma_start(out=x_raw[0][:], in_=x_rows[:, :, half_cols(0)])
        load_plane(shared_planes, WG_ROW, wg_scales)
        nc.sync.dma_start(out=wg_raw[:], in_=wg_words[0].rearrange("p r i -> p (r i)").bitcast(I32))
        nc.sync.dma_start(out=wu_raw[:], in_=wu.rearrange("(p j) r -> p j r", j=PACK))
        nc.sync.dma_start(out=x_raw[1][:], in_=x_rows[:, :, half_cols(1)])
        load_plane(v4_plane, V4_ROW, v4_scales)
        nc.sync.dma_start(out=g_sb[:], in_=g_rows)
        nc.sync.dma_start(out=v4_codes[:].bitcast(I32), in_=v4_words[0].bitcast(I32))
        nc.sync.dma_start(out=v8_codes[:].bitcast(I32), in_=v8_words[0].rearrange("p n i -> p (n i)").bitcast(I32))

        interleave(nc.vector.tensor_copy, x_bf[0], x_raw[0], 0, CHUNK)
        interleave(nc.scalar.copy, x_bf[0], x_raw[0], CHUNK, HALF)
        deal(wg_plane, shared_planes)
        quantize_x(0)
        load_plane(shared_planes, V8_ROW, v8_scales)
        deal(wg_codes, wg_raw)
        quantize_x(1)
        for step in FIRST_STEPS:
            sigmoid(step, gate_sums(step))

        for pair in range(2):
            round_wu(pair)
        for pair in range(2):
            quantize_wu(pair)
        first_ub = {step: up_sums(step) for step in FIRST_STEPS}

        interleave(nc.vector.tensor_copy, x_bf[1], x_raw[1], 0, PIECE)
        interleave(nc.scalar.copy, x_bf[1], x_raw[1], PIECE, CHUNK)
        interleave(nc.scalar.copy, x_bf[1], x_raw[1], CHUNK, HALF)

        for chunk in range(2):
            for pair in range(2):
                hidden((chunk, pair), first_ub[(chunk, pair)])
            if chunk == 1:
                store_h(slice(0, PACK), 0)
            quantize_x(chunk + 2)
            round_h_gpsimd(chunk)
        round_h_scalar(0)
        for pair in range(2):
            whole_step((2, pair))
        round_h_scalar(1)
        round_h_gpsimd(2)
        quantize_h(0, 2)
        store_words(0)
        for pair in range(2):
            whole_step((3, pair))
            store_h(pair_rows(pair), 1)
        round_h_scalar(2)
        round_h_gpsimd(3)
        round_h_scalar(3)

        for block in (0, 1):
            last_layer(0, block)
        store_y(slice(0, 2), half_cols(0))
        quantize_h(2, 1)
        quantize_h(3, 1)
        store_words(1)

        for block in (2, 3):
            last_layer(0, block)
        for block in (2, 3):
            last_layer(1, block)
            store_y(slice(block, block + 1), slice(0, T))
        for block in (0, 1):
            last_layer(1, block)
        store_y(slice(0, 2), half_cols(1))

        for quad in range(QUADS):
            nc.sync.dma_start(
                out=out_3[0, 4 * quad : 4 * quad + 4, :].bitcast(I32),
                in_=h_plane[32 * quad : 32 * quad + 4, :].bitcast(I32),
            )
